import numpy as np
import ml_dtypes


def mxq(x, axis, fmt="e4m3"):
    dtype, down = {"e4m3": (ml_dtypes.float8_e4m3fn, 7), "e5m2": (ml_dtypes.float8_e5m2, 14)}[fmt]
    v = np.moveaxis(np.asarray(x, np.float32).astype(ml_dtypes.bfloat16).astype(np.float64), axis, -1)
    blocks = v.reshape(v.shape[:-1] + (-1, 32))
    amax = np.abs(blocks).max(-1, keepdims=True)
    byte = np.maximum(np.where(amax > 0, np.frexp(amax)[1] - 1 + 127, 0) - down, 1)
    scale = np.exp2(byte - 127.0)
    codes = (blocks / scale).astype(np.float32).astype(dtype).astype(np.float64)
    return np.moveaxis((codes * scale).reshape(v.shape), -1, axis)


WIDE = False


def mx_kscale(k):
    if not WIDE:
        return np.ones(k)
    levels = np.array([18, -18])
    if k % 512:
        return np.exp2(np.random.permutation(np.resize(levels, k // 32))).repeat(32)
    a = np.empty((k // 512, 16))
    for p in range(k // 512):
        a[p, :8] = np.random.permutation(np.resize(levels, 8))
        for g in range(8):
            far = levels[np.abs(levels - a[p, g]) >= 10]
            a[p, g + 8] = far[np.random.randint(len(far))]
    return np.exp2(a.ravel()).repeat(32)


def f64(x):
    return np.asarray(x).astype(np.float64)


def striped(idx):
    return np.tile(np.asarray(idx).reshape(-1, 16).T, (8, 1)).astype(np.uint16)


def unstriped(offs):
    return offs[:16].T.reshape(-1).astype(np.int64)


B, N, T, D, DV, R = 1, 512, 2048, 512, 512, 512
PAGE = 64


def setup_inputs():
    n = np.random.standard_normal
    pages = np.random.permutation(T // PAGE)[:B * N // PAGE]
    idx = (pages[:, None] * PAGE + np.arange(PAGE)[None, :]).reshape(-1)
    s = mx_kscale(D)[:, None]
    z = mx_kscale(R)[:, None]
    v = mx_kscale(DV)[:, None]
    q = n((B, D, R))
    do = n((B, DV, R))
    return {
        "qT": (q * s).astype(np.float32),
        "kT": (n((D, T)) * (0.50 / np.sqrt(D)) / s).astype(np.float32),
        "vT": (n((DV, T)) / np.sqrt(DV) / v).astype(np.float32),
        "doT": (do * v).astype(np.float32),
        "rw": (np.random.uniform(0.5, 1.5, (B, R, 1)) * 1.0 / np.sqrt(R) * z).astype(np.float32),
        "qm": (q.transpose(0, 2, 1) / z).astype(np.float32),
        "offs": striped(idx),
    }


def reference(qT, kT, vT, doT, rw, qm, offs):
    idx = unstriped(offs)
    pick = lambda x: x[:, idx].reshape(x.shape[0], B, N).transpose(1, 0, 2)
    a = mxq(f64(qT), 1, "e4m3").transpose(0, 2, 1) @ mxq(pick(f64(kT)), 1, "e4m3")
    p = np.exp(a)
    dp = mxq(f64(doT), 1, "e5m2").transpose(0, 2, 1) @ mxq(pick(f64(vT)), 1, "e4m3")
    ds = f64(rw) * dp * p
    dk = mxq(f64(qm), 1, "e4m3").transpose(0, 2, 1) @ mxq(ds, 1, "e5m2")
    gk = np.zeros((D, T))
    gk[:, idx] = dk.transpose(1, 0, 2).reshape(D, B * N)
    return gk

@@ -1,0 +1,156 @@
+from contextlib import ExitStack
+
+import concourse.mybir as mybir
+
+N, T, D, R = 512, 2048, 512, 512
+FLOPS = 3 * 2 * N * D * R
+
+F32 = mybir.dt.float32
+BF16 = mybir.dt.bfloat16
+U32 = mybir.dt.uint32
+U16 = mybir.dt.uint16
+U8 = mybir.dt.uint8
+E4 = mybir.dt.float8_e4m3fn_x4
+E5 = mybir.dt.float8_e5m2_x4
+ACT = mybir.ActivationFunctionType
+MULT = mybir.AluOpType.mult
+
+P = 128
+PACK = 4
+CHUNK = 128
+HALF = N // 2
+STRIPE = 16
+
+
+def tile_attend_gat_exp_k_kernel(tc, qT, kT, vT, doT, rw, qm, offs, out):
+    nc = tc.nc
+    with ExitStack() as ctx:
+        keep = ctx.enter_context(tc.tile_pool(name="keep", bufs=1))
+        ring = ctx.enter_context(tc.tile_pool(name="ring", bufs=4))
+        psum = ctx.enter_context(tc.psum_pool(name="psum", bufs=4))
+
+        def mx_pair(name, width):
+            codes = keep.tile([P, width], U32, name=name + "_codes", align_bytes=64)
+            scales = keep.tile([P, width], U8, name=name + "_scales", align_bytes=64)
+            return codes, scales
+
+        def quantize(pair, cols, grouped, fmt):
+            nc.vector.quantize_mx(out=pair[0][:, cols].bitcast(fmt), scales=pair[1][:, cols], in_=grouped)
+
+        def multiply(acc, left, left_cols, left_fmt, right, right_cols, right_fmt):
+            nc.tensor.matmul_mx(
+                out=acc,
+                lhsT=left[0][:, left_cols].bitcast(left_fmt),
+                lhsT_scale=left[1][:, left_cols],
+                rhs=right[0][:, right_cols].bitcast(right_fmt),
+                rhs_scale=right[1][:, right_cols],
+                start=True,
+                stop=True,
+            )
+
+        def slots(lo, hi):
+            return offsets[:, lo // STRIPE : hi // STRIPE]
+
+        offsets = keep.tile([P, N // STRIPE], U16, name="offsets")
+        gate = keep.tile([P, PACK], F32, name="gate")
+        do_raw = keep.tile([P, PACK, R], F32, name="do_raw")
+        q_raw = keep.tile([P, PACK, R], F32, name="q_raw")
+        v_pool = [keep.tile([P, T], F32, name="v_pool%d" % j) for j in range(PACK)]
+        k_pool = [keep.tile([P, T], F32, name="k_pool%d" % j) for j in range(PACK)]
+        qm_first = keep.tile([P, PACK, P], F32, name="qm_first")
+        qm_rest = keep.tile([P, PACK, D - P], F32, name="qm_rest")
+        v_rows = vT.rearrange("(p j) n -> p j n", j=PACK)
+        k_rows = kT.rearrange("(p j) n -> p j n", j=PACK)
+        qm_rows = qm[0].rearrange("(p j) d -> p j d", j=PACK)
+
+        nc.sync.dma_start(do_raw[:], doT[0].rearrange("(p j) r -> p j r", j=PACK))
+        nc.sync.dma_start(offsets[:], offs)
+        nc.sync.dma_start(gate[:], rw[0].rearrange("(p t) o -> p (t o)", t=PACK))
+        for j in range(PACK):
+            nc.sync.dma_start(v_pool[j][:], v_rows[:, j, :])
+        nc.sync.dma_start(q_raw[:], qT[0].rearrange("(p j) r -> p j r", j=PACK))
+        for j in range(PACK):
+            nc.sync.dma_start(k_pool[j][:], k_rows[:, j, :])
+        nc.sync.dma_start(qm_first[:], qm_rows[:, :, :P])
+        nc.sync.dma_start(qm_rest[:], qm_rows[:, :, P:])
+
+        warm = keep.tile([P, 8], F32, name="warm")
+        warm_out = keep.tile([P, 8], F32, name="warm_out")
+        nc.vector.memset(warm[:], 0.0)
+        nc.scalar.activation(warm_out[:], warm[:], ACT.Exp)
+        windows = [keep.tile([P, T], F32, name="window%d" % b) for b in range(D // P)]
+        for window in windows:
+            nc.vector.memset(window[:], 0.0)
+
+        def group_queries(raw, name):
+            grouped = keep.tile([P, PACK, P, PACK], BF16, name=name, align_bytes=64)
+            nc.scalar.copy(
+                grouped[:].rearrange("p t m j -> p m t j"),
+                raw[:].rearrange("p j (m t) -> p m t j", t=PACK),
+            )
+            return grouped[:].rearrange("p t m j -> p (t m j)")
+
+        everything = slice(0, N)
+
+        do_mx = mx_pair("do", R)
+        quantize(do_mx, everything, group_queries(do_raw, "do_grouped"), E5)
+        v_grouped = keep.tile([P, N, PACK], BF16, name="v_grouped", align_bytes=64)
+        for j in range(PACK):
+            nc.vector.tensor_copy(v_grouped[:, :, j], v_pool[j][:].indirect(offsets[:]))
+        v_mx = mx_pair("v", N)
+        quantize(v_mx, everything, v_grouped[:].rearrange("p i j -> p (i j)"), E4)
+        gated = keep.tile([P, PACK, N], F32, name="gated")
+        for t in range(PACK):
+            dp = psum.tile([P, N], F32, name="dp", tag="wide")
+            multiply(dp[:], do_mx, slice(t * P, (t + 1) * P), E5, v_mx, everything, E4)
+            nc.scalar.activation(gated[:, t, :], dp[:], ACT.Copy, scale=gate[:, t : t + 1])
+        q_mx = mx_pair("q", R)
+        quantize(q_mx, everything, group_queries(q_raw, "q_grouped"), E4)
+        gated_grouped = keep.tile([P, N, PACK], F32, name="gated_grouped")
+        nc.scalar.copy(gated_grouped[:], gated[:].rearrange("p t i -> p i t"))
+
+        k_grouped = keep.tile([P, N, PACK], BF16, name="k_grouped", align_bytes=64)
+        for j in range(PACK - 1):
+            nc.vector.tensor_copy(k_grouped[:, :, j], k_pool[j][:].indirect(offsets[:]))
+        k_mx = mx_pair("k", N)
+        for lo in range(0, N, HALF):
+            nc.vector.tensor_copy(
+                k_grouped[:, lo : lo + HALF, PACK - 1], k_pool[PACK - 1][:].indirect(slots(lo, lo + HALF))
+            )
+            quantize(
+                k_mx, slice(lo, lo + HALF), k_grouped[:, lo : lo + HALF, :].rearrange("p i j -> p (i j)"), E4
+            )
+
+        qm_mx = mx_pair("qm", D)
+
+        def quantize_qm(b, grouped):
+            raw = qm_first[:] if b == 0 else qm_rest[:, :, (b - 1) * P : b * P]
+            nc.scalar.copy(grouped[:], raw.rearrange("p j d -> p d j"))
+            quantize(qm_mx, slice(b * P, (b + 1) * P), grouped[:].rearrange("p d j -> p (d j)"), E4)
+
+        ds_grouped = keep.tile([P, N, PACK], BF16, name="ds_grouped", align_bytes=64)
+        ds_mx = mx_pair("ds", N)
+        for lo in range(0, N, CHUNK):
+            cols = slice(lo, lo + CHUNK)
+            scores = psum.tile([P, PACK, CHUNK], F32, name="scores")
+            for t in range(PACK):
+                multiply(scores[:, t, :], q_mx, slice(t * P, (t + 1) * P), E4, k_mx, cols, E4)
+            weights = ring.tile([P, CHUNK, PACK], F32, name="weights", tag="late", align_bytes=64)
+            nc.scalar.activation(weights[:], scores[:].rearrange("p t i -> p i t"), ACT.Exp)
+            nc.vector.tensor_tensor(ds_grouped[:, cols, :], weights[:], gated_grouped[:, cols, :], MULT)
+            quantize(ds_mx, cols, ds_grouped[:, cols, :].rearrange("p i t -> p (i t)"), E5)
+
+        qm_grouped0 = keep.tile([P, P, PACK], BF16, name="qm_grouped0", align_bytes=64)
+        quantize_qm(0, qm_grouped0)
+
+        for b in range(D // P):
+            if b > 0:
+                qm_grouped = ring.tile([P, P, PACK], BF16, name="qm_grouped", tag="late", align_bytes=64)
+                quantize_qm(b, qm_grouped)
+            dk = psum.tile([P, N], F32, name="dk", tag="wide")
+            multiply(dk[:], qm_mx, slice(b * P, (b + 1) * P), E4, ds_mx, everything, E5)
+            for lo in range(0, N, HALF):
+                dk_half = ring.tile([P, HALF], F32, name="dk_half", bufs=8)
+                nc.scalar.copy(dk_half[:], dk[:, lo : lo + HALF])
+                nc.vector.tensor_copy(windows[b][:].indirect(slots(lo, lo + HALF)), dk_half[:])
+            nc.sync.dma_start(out[b * P : (b + 1) * P, :], windows[b][:])

@@ -17,7 +17,8 @@ MULT = mybir.AluOpType.mult
 
 P = 128
 PACK = 4
-CHUNK = 128
+CHUNKS = (128, 128, 128, 128)
+RUN = 4
 HALF = N // 2
 STRIPE = 16
 
@@ -27,7 +28,7 @@ def tile_attend_gat_exp_k_kernel(tc, qT, kT, vT, doT, rw, qm, offs, out):
     with ExitStack() as ctx:
         keep = ctx.enter_context(tc.tile_pool(name="keep", bufs=1))
         ring = ctx.enter_context(tc.tile_pool(name="ring", bufs=4))
-        psum = ctx.enter_context(tc.psum_pool(name="psum", bufs=4))
+        psum = ctx.enter_context(tc.psum_pool(name="psum", bufs=1))
 
         def mx_pair(name, width):
             codes = keep.tile([P, width], U32, name=name + "_codes", align_bytes=64)
@@ -82,41 +83,54 @@ def tile_attend_gat_exp_k_kernel(tc, qT, kT, vT, doT, rw, qm, offs, out):
         for window in windows:
             nc.vector.memset(window[:], 0.0)
 
-        def group_queries(raw, name):
+        def interleave(copy, grouped, planes):
+            copy(
+                grouped.rearrange("p (c i) j -> p c j i", i=RUN),
+                planes.rearrange("p j (c i) -> p c j i", i=RUN),
+            )
+
+        def group_queries(copy, raw, name):
             grouped = keep.tile([P, PACK, P, PACK], BF16, name=name, align_bytes=64)
-            nc.scalar.copy(
-                grouped[:].rearrange("p t m j -> p m t j"),
-                raw[:].rearrange("p j (m t) -> p m t j", t=PACK),
+            copy(
+                grouped[:].rearrange("p t m j -> p m j t"),
+                raw[:].rearrange("p j (m t) -> p m j t", t=PACK),
             )
             return grouped[:].rearrange("p t m j -> p (t m j)")
 
         everything = slice(0, N)
 
         do_mx = mx_pair("do", R)
-        quantize(do_mx, everything, group_queries(do_raw, "do_grouped"), E5)
+        quantize(do_mx, everything, group_queries(nc.scalar.copy, do_raw, "do_grouped"), E5)
         v_grouped = keep.tile([P, N, PACK], BF16, name="v_grouped", align_bytes=64)
+        v_listed = keep.tile([P, PACK, N], F32, name="v_listed")
         for j in range(PACK):
-            nc.vector.tensor_copy(v_grouped[:, :, j], v_pool[j][:].indirect(offsets[:]))
+            nc.vector.tensor_copy(v_listed[:, j, :], v_pool[j][:].indirect(offsets[:]))
+        interleave(nc.vector.tensor_copy, v_grouped[:], v_listed[:])
         v_mx = mx_pair("v", N)
         quantize(v_mx, everything, v_grouped[:].rearrange("p i j -> p (i j)"), E4)
         gated = keep.tile([P, PACK, N], F32, name="gated")
         for t in range(PACK):
-            dp = psum.tile([P, N], F32, name="dp", tag="wide")
+            dp = psum.tile([P, N], F32, name="dp", tag="wide", bufs=4)
             multiply(dp[:], do_mx, slice(t * P, (t + 1) * P), E5, v_mx, everything, E4)
             nc.scalar.activation(gated[:, t, :], dp[:], ACT.Copy, scale=gate[:, t : t + 1])
         q_mx = mx_pair("q", R)
-        quantize(q_mx, everything, group_queries(q_raw, "q_grouped"), E4)
+        quantize(q_mx, everything, group_queries(nc.vector.tensor_copy, q_raw, "q_grouped"), E4)
         gated_grouped = keep.tile([P, N, PACK], F32, name="gated_grouped")
-        nc.scalar.copy(gated_grouped[:], gated[:].rearrange("p t i -> p i t"))
+        interleave(nc.scalar.copy, gated_grouped[:], gated[:])
 
         k_grouped = keep.tile([P, N, PACK], BF16, name="k_grouped", align_bytes=64)
+        k_listed = keep.tile([P, PACK, N], F32, name="k_listed")
         for j in range(PACK - 1):
-            nc.vector.tensor_copy(k_grouped[:, :, j], k_pool[j][:].indirect(offsets[:]))
+            nc.vector.tensor_copy(k_listed[:, j, :], k_pool[j][:].indirect(offsets[:]))
+            if j == 1:
+                nc.vector.tensor_copy(k_grouped[:, :, 0:2], k_listed[:, 0:2, :].rearrange("p j i -> p i j"))
         k_mx = mx_pair("k", N)
         for lo in range(0, N, HALF):
             nc.vector.tensor_copy(
-                k_grouped[:, lo : lo + HALF, PACK - 1], k_pool[PACK - 1][:].indirect(slots(lo, lo + HALF))
+                k_listed[:, PACK - 1, lo : lo + HALF], k_pool[PACK - 1][:].indirect(slots(lo, lo + HALF))
             )
+        for lo, copy in ((0, nc.vector.tensor_copy), (HALF, nc.scalar.copy)):
+            copy(k_grouped[:, lo : lo + HALF, 2:4], k_listed[:, 2:4, lo : lo + HALF].rearrange("p j i -> p i j"))
             quantize(
                 k_mx, slice(lo, lo + HALF), k_grouped[:, lo : lo + HALF, :].rearrange("p i j -> p (i j)"), E4
             )
@@ -125,17 +139,18 @@ def tile_attend_gat_exp_k_kernel(tc, qT, kT, vT, doT, rw, qm, offs, out):
 
         def quantize_qm(b, grouped):
             raw = qm_first[:] if b == 0 else qm_rest[:, :, (b - 1) * P : b * P]
-            nc.scalar.copy(grouped[:], raw.rearrange("p j d -> p d j"))
+            interleave(nc.scalar.copy, grouped[:], raw)
             quantize(qm_mx, slice(b * P, (b + 1) * P), grouped[:].rearrange("p d j -> p (d j)"), E4)
 
-        ds_grouped = keep.tile([P, N, PACK], BF16, name="ds_grouped", align_bytes=64)
+        ds_grouped = keep.tile([P, N, PACK], BF16, name="ds_grouped", tag="tail", align_bytes=64)
         ds_mx = mx_pair("ds", N)
-        for lo in range(0, N, CHUNK):
-            cols = slice(lo, lo + CHUNK)
-            scores = psum.tile([P, PACK, CHUNK], F32, name="scores")
+        for c, width in enumerate(CHUNKS):
+            lo = sum(CHUNKS[:c])
+            cols = slice(lo, lo + width)
+            scores = psum.tile([P, PACK, width], F32, name="scores", bufs=len(CHUNKS))
             for t in range(PACK):
                 multiply(scores[:, t, :], q_mx, slice(t * P, (t + 1) * P), E4, k_mx, cols, E4)
-            weights = ring.tile([P, CHUNK, PACK], F32, name="weights", tag="late", align_bytes=64)
+            weights = ring.tile([P, width, PACK], F32, name="weights", bufs=len(CHUNKS))
             nc.scalar.activation(weights[:], scores[:].rearrange("p t i -> p i t"), ACT.Exp)
             nc.vector.tensor_tensor(ds_grouped[:, cols, :], weights[:], gated_grouped[:, cols, :], MULT)
             quantize(ds_mx, cols, ds_grouped[:, cols, :].rearrange("p i t -> p (i t)"), E5)
@@ -145,9 +160,9 @@ def tile_attend_gat_exp_k_kernel(tc, qT, kT, vT, doT, rw, qm, offs, out):
 
         for b in range(D // P):
             if b > 0:
-                qm_grouped = ring.tile([P, P, PACK], BF16, name="qm_grouped", tag="late", align_bytes=64)
+                qm_grouped = keep.tile([P, P, PACK], BF16, name="qm_grouped", tag="tail", align_bytes=64)
                 quantize_qm(b, qm_grouped)
-            dk = psum.tile([P, N], F32, name="dk", tag="wide")
+            dk = psum.tile([P, N], F32, name="dk", tag="wide", bufs=4)
             multiply(dk[:], qm_mx, slice(b * P, (b + 1) * P), E4, ds_mx, everything, E5)
             for lo in range(0, N, HALF):
                 dk_half = ring.tile([P, HALF], F32, name="dk_half", bufs=8)

@@ -21,17 +21,17 @@ CHUNKS = (128, 128, 128, 128)
 RUN = 4
 HALF = N // 2
 STRIPE = 16
+Q_SPLIT = 68
 
 
 def tile_attend_gat_exp_k_kernel(tc, qT, kT, vT, doT, rw, qm, offs, out):
     nc = tc.nc
     with ExitStack() as ctx:
         keep = ctx.enter_context(tc.tile_pool(name="keep", bufs=1))
-        ring = ctx.enter_context(tc.tile_pool(name="ring", bufs=4))
         psum = ctx.enter_context(tc.psum_pool(name="psum", bufs=1))
 
-        def mx_pair(name, width):
-            codes = keep.tile([P, width], U32, name=name + "_codes", align_bytes=64)
+        def mx_pair(name, width, tag=None):
+            codes = keep.tile([P, width], U32, name=name + "_codes", tag=tag or name + "_codes", align_bytes=64)
             scales = keep.tile([P, width], U8, name=name + "_scales", align_bytes=64)
             return codes, scales
 
@@ -55,11 +55,11 @@ def tile_attend_gat_exp_k_kernel(tc, qT, kT, vT, doT, rw, qm, offs, out):
         offsets = keep.tile([P, N // STRIPE], U16, name="offsets")
         gate = keep.tile([P, PACK], F32, name="gate")
         do_raw = keep.tile([P, PACK, R], F32, name="do_raw")
-        q_raw = keep.tile([P, PACK, R], F32, name="q_raw")
+        q_raw = keep.tile([P, PACK, R], F32, name="q_raw", tag="q_raw", align_bytes=64)
         v_pool = [keep.tile([P, T], F32, name="v_pool%d" % j) for j in range(PACK)]
         k_pool = [keep.tile([P, T], F32, name="k_pool%d" % j) for j in range(PACK)]
-        qm_first = keep.tile([P, PACK, P], F32, name="qm_first")
-        qm_rest = keep.tile([P, PACK, D - P], F32, name="qm_rest")
+        qm_first = keep.tile([P, PACK, 2 * P], F32, name="qm_first")
+        qm_rest = keep.tile([P, PACK, 2 * P], F32, name="qm_rest")
         v_rows = vT.rearrange("(p j) n -> p j n", j=PACK)
         k_rows = kT.rearrange("(p j) n -> p j n", j=PACK)
         qm_rows = qm[0].rearrange("(p j) d -> p j d", j=PACK)
@@ -69,19 +69,22 @@ def tile_attend_gat_exp_k_kernel(tc, qT, kT, vT, doT, rw, qm, offs, out):
         nc.sync.dma_start(gate[:], rw[0].rearrange("(p t) o -> p (t o)", t=PACK))
         for j in range(PACK):
             nc.sync.dma_start(v_pool[j][:], v_rows[:, j, :])
-        nc.sync.dma_start(q_raw[:], qT[0].rearrange("(p j) r -> p j r", j=PACK))
         for j in range(PACK):
             nc.sync.dma_start(k_pool[j][:], k_rows[:, j, :])
-        nc.sync.dma_start(qm_first[:], qm_rows[:, :, :P])
-        nc.sync.dma_start(qm_rest[:], qm_rows[:, :, P:])
+        nc.sync.dma_start(q_raw[:], qT[0].rearrange("(p j) r -> p j r", j=PACK))
+        nc.sync.dma_start(qm_first[:], qm_rows[:, :, : 2 * P])
+        nc.sync.dma_start(qm_rest[:], qm_rows[:, :, 2 * P :])
 
         warm = keep.tile([P, 8], F32, name="warm")
         warm_out = keep.tile([P, 8], F32, name="warm_out")
         nc.vector.memset(warm[:], 0.0)
         nc.scalar.activation(warm_out[:], warm[:], ACT.Exp)
+        ds_mx = mx_pair("ds", HALF + N)
+        nc.vector.memset(ds_mx[0][:, :HALF], 0)
+        nc.vector.memset(ds_mx[1][:, :HALF], 0)
         windows = [keep.tile([P, T], F32, name="window%d" % b) for b in range(D // P)]
-        for window in windows:
-            nc.vector.memset(window[:], 0.0)
+        for b, window in enumerate(windows):
+            (nc.vector, nc.gpsimd)[b % 2].memset(window[:], 0.0)
 
         def interleave(copy, grouped, planes):
             copy(
@@ -89,23 +92,28 @@ def tile_attend_gat_exp_k_kernel(tc, qT, kT, vT, doT, rw, qm, offs, out):
                 planes.rearrange("p j (c i) -> p c j i", i=RUN),
             )
 
-        def group_queries(copy, raw, name):
-            grouped = keep.tile([P, PACK, P, PACK], BF16, name=name, align_bytes=64)
-            copy(
-                grouped[:].rearrange("p t m j -> p m j t"),
-                raw[:].rearrange("p j (m t) -> p m j t", t=PACK),
-            )
-            return grouped[:].rearrange("p t m j -> p (t m j)")
+        def group_queries(shares, raw, name):
+            grouped = keep.tile([P, PACK, P, PACK], BF16, name=name, tag=name, align_bytes=64)
+            for copy, lo, hi in shares:
+                copy(
+                    grouped[:, :, lo:hi, :].rearrange("p t m j -> p m j t"),
+                    raw[:, :, lo * PACK : hi * PACK].rearrange("p j (m t) -> p m j t", t=PACK),
+                )
+            return grouped
 
         everything = slice(0, N)
 
         do_mx = mx_pair("do", R)
-        quantize(do_mx, everything, group_queries(nc.scalar.copy, do_raw, "do_grouped"), E5)
-        v_grouped = keep.tile([P, N, PACK], BF16, name="v_grouped", align_bytes=64)
+        do_grouped = group_queries([(nc.scalar.copy, 0, P)], do_raw, "do_grouped")
+        quantize(do_mx, everything, do_grouped[:].rearrange("p t m j -> p (t m j)"), E5)
+        v_grouped = keep.tile([P, N, PACK], BF16, name="v_grouped", tag="pools", align_bytes=64)
         v_listed = keep.tile([P, PACK, N], F32, name="v_listed")
         for j in range(PACK):
             nc.vector.tensor_copy(v_listed[:, j, :], v_pool[j][:].indirect(offsets[:]))
-        interleave(nc.vector.tensor_copy, v_grouped[:], v_listed[:])
+            if j % 2 == 1:
+                nc.vector.tensor_copy(
+                    v_grouped[:, :, j - 1 : j + 1], v_listed[:, j - 1 : j + 1, :].rearrange("p j i -> p i j")
+                )
         v_mx = mx_pair("v", N)
         quantize(v_mx, everything, v_grouped[:].rearrange("p i j -> p (i j)"), E4)
         gated = keep.tile([P, PACK, N], F32, name="gated")
@@ -113,59 +121,82 @@ def tile_attend_gat_exp_k_kernel(tc, qT, kT, vT, doT, rw, qm, offs, out):
             dp = psum.tile([P, N], F32, name="dp", tag="wide", bufs=4)
             multiply(dp[:], do_mx, slice(t * P, (t + 1) * P), E5, v_mx, everything, E4)
             nc.scalar.activation(gated[:, t, :], dp[:], ACT.Copy, scale=gate[:, t : t + 1])
-        q_mx = mx_pair("q", R)
-        quantize(q_mx, everything, group_queries(nc.vector.tensor_copy, q_raw, "q_grouped"), E4)
         gated_grouped = keep.tile([P, N, PACK], F32, name="gated_grouped")
         interleave(nc.scalar.copy, gated_grouped[:], gated[:])
 
         k_grouped = keep.tile([P, N, PACK], BF16, name="k_grouped", align_bytes=64)
-        k_listed = keep.tile([P, PACK, N], F32, name="k_listed")
+        k_listed = keep.tile([P, PACK, N], F32, name="k_listed", tag="pools", align_bytes=64)
         for j in range(PACK - 1):
             nc.vector.tensor_copy(k_listed[:, j, :], k_pool[j][:].indirect(offsets[:]))
             if j == 1:
                 nc.vector.tensor_copy(k_grouped[:, :, 0:2], k_listed[:, 0:2, :].rearrange("p j i -> p i j"))
-        k_mx = mx_pair("k", N)
         for lo in range(0, N, HALF):
             nc.vector.tensor_copy(
                 k_listed[:, PACK - 1, lo : lo + HALF], k_pool[PACK - 1][:].indirect(slots(lo, lo + HALF))
             )
-        for lo, copy in ((0, nc.vector.tensor_copy), (HALF, nc.scalar.copy)):
+        for lo, copy in ((0, nc.scalar.copy), (HALF, nc.vector.tensor_copy)):
             copy(k_grouped[:, lo : lo + HALF, 2:4], k_listed[:, 2:4, lo : lo + HALF].rearrange("p j i -> p i j"))
-            quantize(
-                k_mx, slice(lo, lo + HALF), k_grouped[:, lo : lo + HALF, :].rearrange("p i j -> p (i j)"), E4
-            )
 
-        qm_mx = mx_pair("qm", D)
+        def quantize_keys(lo, codes_tag):
+            pair = mx_pair("k%d" % lo, HALF, codes_tag)
+            quantize(pair, slice(0, HALF), k_grouped[:, lo : lo + HALF, :].rearrange("p i j -> p (i j)"), E4)
+            return pair
 
-        def quantize_qm(b, grouped):
-            raw = qm_first[:] if b == 0 else qm_rest[:, :, (b - 1) * P : b * P]
-            interleave(nc.scalar.copy, grouped[:], raw)
-            quantize(qm_mx, slice(b * P, (b + 1) * P), grouped[:].rearrange("p d j -> p (d j)"), E4)
+        k_mx = [quantize_keys(0, None)]
 
-        ds_grouped = keep.tile([P, N, PACK], BF16, name="ds_grouped", tag="tail", align_bytes=64)
-        ds_mx = mx_pair("ds", N)
+        q_mx = mx_pair("q", R)
+        q_grouped = group_queries(
+            [(nc.vector.tensor_copy, 0, Q_SPLIT), (nc.scalar.copy, Q_SPLIT, P)], q_raw, "q_grouped"
+        )
+        for t in range(PACK):
+            quantize(q_mx, slice(t * P, (t + 1) * P), q_grouped[:, t].rearrange("p m j -> p (m j)"), E4)
+        k_mx.append(quantize_keys(HALF, "q_raw"))
+
+        qm_mx = {}
+
+        def quantize_qm(b, tag, copy, codes_tag=None):
+            grouped = keep.tile([P, P, PACK], BF16, name="qm_grouped", tag=tag, align_bytes=64)
+            raw = (qm_first, qm_rest)[b // 2][:, :, b % 2 * P : (b % 2 + 1) * P]
+            interleave(copy, grouped[:], raw)
+            qm_mx[b] = mx_pair("qm%d" % b, P, codes_tag)
+            quantize(qm_mx[b], slice(0, P), grouped[:].rearrange("p d j -> p (d j)"), E4)
+
+        def scatter(b, dk, lo, hi, tag):
+            staged = keep.tile([P, hi - lo], F32, name="staged", tag=tag, align_bytes=64)
+            nc.scalar.copy(staged[:], dk)
+            nc.vector.tensor_copy(windows[b][:].indirect(slots(lo, hi)), staged[:])
+
+        def dk_pass(b, first):
+            dk = psum.tile([P, N], F32, name="dk", tag="wide", bufs=4)
+            multiply(dk[:], qm_mx[b], slice(0, P), E4, ds_mx, slice(first, first + N), E5)
+            return dk
+
+        ds_grouped = keep.tile([P, N, PACK], BF16, name="ds_grouped", tag="ds_grouped", align_bytes=64)
         for c, width in enumerate(CHUNKS):
             lo = sum(CHUNKS[:c])
             cols = slice(lo, lo + width)
+            key_cols = slice(lo % HALF, lo % HALF + width)
             scores = psum.tile([P, PACK, width], F32, name="scores", bufs=len(CHUNKS))
             for t in range(PACK):
-                multiply(scores[:, t, :], q_mx, slice(t * P, (t + 1) * P), E4, k_mx, cols, E4)
-            weights = ring.tile([P, width, PACK], F32, name="weights", bufs=len(CHUNKS))
+                multiply(scores[:, t, :], q_mx, slice(t * P, (t + 1) * P), E4, k_mx[lo // HALF], key_cols, E4)
+            weights = keep.tile([P, width, PACK], F32, name="weights", tag="weights%d" % c, align_bytes=64)
             nc.scalar.activation(weights[:], scores[:].rearrange("p t i -> p i t"), ACT.Exp)
+            if c == 0:
+                quantize_qm(0, "qm0", nc.scalar.copy)
+                quantize_qm(1, "q_grouped", nc.vector.tensor_copy)
             nc.vector.tensor_tensor(ds_grouped[:, cols, :], weights[:], gated_grouped[:, cols, :], MULT)
-            quantize(ds_mx, cols, ds_grouped[:, cols, :].rearrange("p i t -> p (i t)"), E5)
+            quantize(
+                ds_mx,
+                slice(HALF + lo, HALF + lo + width),
+                ds_grouped[:, cols, :].rearrange("p i t -> p (i t)"),
+                E5,
+            )
 
-        qm_grouped0 = keep.tile([P, P, PACK], BF16, name="qm_grouped0", align_bytes=64)
-        quantize_qm(0, qm_grouped0)
-
-        for b in range(D // P):
-            if b > 0:
-                qm_grouped = keep.tile([P, P, PACK], BF16, name="qm_grouped", tag="tail", align_bytes=64)
-                quantize_qm(b, qm_grouped)
-            dk = psum.tile([P, N], F32, name="dk", tag="wide", bufs=4)
-            multiply(dk[:], qm_mx, slice(b * P, (b + 1) * P), E4, ds_mx, everything, E5)
-            for lo in range(0, N, HALF):
-                dk_half = ring.tile([P, HALF], F32, name="dk_half", bufs=8)
-                nc.scalar.copy(dk_half[:], dk[:, lo : lo + HALF])
-                nc.vector.tensor_copy(windows[b][:].indirect(slots(lo, lo + HALF)), dk_half[:])
+        scatter(0, dk_pass(0, 0)[:, HALF:], 0, HALF, "early")
+        scatter(0, dk_pass(0, HALF)[:, HALF:], HALF, N, "late")
+        nc.sync.dma_start(out[:P, :], windows[0][:])
+        for b, tag, codes_tag in ((1, None, None), (2, "weights0", "ds_grouped"), (3, "late", None)):
+            if tag:
+                quantize_qm(b, tag, nc.scalar.copy, codes_tag)
+            scatter(b, dk_pass(b, HALF)[:], 0, N, "staged%d" % b)
             nc.sync.dma_start(out[b * P : (b + 1) * P, :], windows[b][:])

@@ -21,7 +21,7 @@ CHUNKS = (128, 128, 128, 128)
 RUN = 4
 HALF = N // 2
 STRIPE = 16
-Q_SPLIT = 68
+Q_SPLIT = 64
 
 
 def tile_attend_gat_exp_k_kernel(tc, qT, kT, vT, doT, rw, qm, offs, out):
@@ -55,7 +55,8 @@ def tile_attend_gat_exp_k_kernel(tc, qT, kT, vT, doT, rw, qm, offs, out):
         offsets = keep.tile([P, N // STRIPE], U16, name="offsets")
         gate = keep.tile([P, PACK], F32, name="gate")
         do_raw = keep.tile([P, PACK, R], F32, name="do_raw")
-        q_raw = keep.tile([P, PACK, R], F32, name="q_raw", tag="q_raw", align_bytes=64)
+        q_early = keep.tile([P, PACK, Q_SPLIT * PACK], F32, name="q_early")
+        q_late = keep.tile([P, PACK, R - Q_SPLIT * PACK], F32, name="q_late", tag="q_raw", align_bytes=64)
         v_pool = [keep.tile([P, T], F32, name="v_pool%d" % j) for j in range(PACK)]
         k_pool = [keep.tile([P, T], F32, name="k_pool%d" % j) for j in range(PACK)]
         qm_first = keep.tile([P, PACK, 2 * P], F32, name="qm_first")
@@ -71,7 +72,9 @@ def tile_attend_gat_exp_k_kernel(tc, qT, kT, vT, doT, rw, qm, offs, out):
             nc.sync.dma_start(v_pool[j][:], v_rows[:, j, :])
         for j in range(PACK):
             nc.sync.dma_start(k_pool[j][:], k_rows[:, j, :])
-        nc.sync.dma_start(q_raw[:], qT[0].rearrange("(p j) r -> p j r", j=PACK))
+        q_rows = qT[0].rearrange("(p j) r -> p j r", j=PACK)
+        nc.sync.dma_start(q_early[:], q_rows[:, :, : Q_SPLIT * PACK])
+        nc.sync.dma_start(q_late[:], q_rows[:, :, Q_SPLIT * PACK :])
         nc.sync.dma_start(qm_first[:], qm_rows[:, :, : 2 * P])
         nc.sync.dma_start(qm_rest[:], qm_rows[:, :, 2 * P :])
 
@@ -92,19 +95,19 @@ def tile_attend_gat_exp_k_kernel(tc, qT, kT, vT, doT, rw, qm, offs, out):
                 planes.rearrange("p j (c i) -> p c j i", i=RUN),
             )
 
-        def group_queries(shares, raw, name):
+        def group_queries(shares, name):
             grouped = keep.tile([P, PACK, P, PACK], BF16, name=name, tag=name, align_bytes=64)
-            for copy, lo, hi in shares:
+            for copy, raw, lo, hi in shares:
                 copy(
                     grouped[:, :, lo:hi, :].rearrange("p t m j -> p m j t"),
-                    raw[:, :, lo * PACK : hi * PACK].rearrange("p j (m t) -> p m j t", t=PACK),
+                    raw[:].rearrange("p j (m t) -> p m j t", t=PACK),
                 )
             return grouped
 
         everything = slice(0, N)
 
         do_mx = mx_pair("do", R)
-        do_grouped = group_queries([(nc.scalar.copy, 0, P)], do_raw, "do_grouped")
+        do_grouped = group_queries([(nc.scalar.copy, do_raw, 0, P)], "do_grouped")
         quantize(do_mx, everything, do_grouped[:].rearrange("p t m j -> p (t m j)"), E5)
         v_grouped = keep.tile([P, N, PACK], BF16, name="v_grouped", tag="pools", align_bytes=64)
         v_listed = keep.tile([P, PACK, N], F32, name="v_listed")
@@ -146,7 +149,7 @@ def tile_attend_gat_exp_k_kernel(tc, qT, kT, vT, doT, rw, qm, offs, out):
 
         q_mx = mx_pair("q", R)
         q_grouped = group_queries(
-            [(nc.vector.tensor_copy, 0, Q_SPLIT), (nc.scalar.copy, Q_SPLIT, P)], q_raw, "q_grouped"
+            [(nc.scalar.copy, q_early, 0, Q_SPLIT), (nc.vector.tensor_copy, q_late, Q_SPLIT, P)], "q_grouped"
         )
         for t in range(PACK):
             quantize(q_mx, slice(t * P, (t + 1) * P), q_grouped[:, t].rearrange("p m j -> p (m j)"), E4)

@@ -14,6 +14,7 @@ E4 = mybir.dt.float8_e4m3fn_x4
 E5 = mybir.dt.float8_e5m2_x4
 ACT = mybir.ActivationFunctionType
 MULT = mybir.AluOpType.mult
+ADD = mybir.AluOpType.add
 
 P = 128
 PACK = 4
@@ -59,7 +60,7 @@ def tile_attend_gat_exp_k_kernel(tc, qT, kT, vT, doT, rw, qm, offs, out):
         q_late = keep.tile([P, PACK, R - Q_SPLIT * PACK], F32, name="q_late", tag="q_raw", align_bytes=64)
         v_pool = [keep.tile([P, T], F32, name="v_pool%d" % j) for j in range(PACK)]
         k_pool = [keep.tile([P, T], F32, name="k_pool%d" % j) for j in range(PACK)]
-        qm_first = keep.tile([P, PACK, 2 * P], F32, name="qm_first")
+        qm_raw = [keep.tile([P, PACK, P], F32, name="qm_raw%d" % b) for b in range(2)]
         qm_rest = keep.tile([P, PACK, 2 * P], F32, name="qm_rest")
         v_rows = vT.rearrange("(p j) n -> p j n", j=PACK)
         k_rows = kT.rearrange("(p j) n -> p j n", j=PACK)
@@ -75,7 +76,8 @@ def tile_attend_gat_exp_k_kernel(tc, qT, kT, vT, doT, rw, qm, offs, out):
         q_rows = qT[0].rearrange("(p j) r -> p j r", j=PACK)
         nc.sync.dma_start(q_early[:], q_rows[:, :, : Q_SPLIT * PACK])
         nc.sync.dma_start(q_late[:], q_rows[:, :, Q_SPLIT * PACK :])
-        nc.sync.dma_start(qm_first[:], qm_rows[:, :, : 2 * P])
+        for b in range(2):
+            nc.sync.dma_start(qm_raw[b][:], qm_rows[:, :, b * P : (b + 1) * P])
         nc.sync.dma_start(qm_rest[:], qm_rows[:, :, 2 * P :])
 
         warm = keep.tile([P, 8], F32, name="warm")
@@ -85,6 +87,8 @@ def tile_attend_gat_exp_k_kernel(tc, qT, kT, vT, doT, rw, qm, offs, out):
         ds_mx = mx_pair("ds", HALF + N)
         nc.vector.memset(ds_mx[0][:, :HALF], 0)
         nc.vector.memset(ds_mx[1][:, :HALF], 0)
+        zeros = keep.tile([P, P], F32, name="zeros")
+        nc.vector.memset(zeros[:], 0.0)
         windows = [keep.tile([P, T], F32, name="window%d" % b) for b in range(D // P)]
         for b, window in enumerate(windows):
             (nc.vector, nc.gpsimd)[b % 2].memset(window[:], 0.0)
@@ -157,17 +161,25 @@ def tile_attend_gat_exp_k_kernel(tc, qT, kT, vT, doT, rw, qm, offs, out):
 
         qm_mx = {}
 
-        def quantize_qm(b, tag, copy, codes_tag=None):
+        qm_grouped = {}
+
+        def group_qm(b, tag, copy):
             grouped = keep.tile([P, P, PACK], BF16, name="qm_grouped", tag=tag, align_bytes=64)
-            raw = (qm_first, qm_rest)[b // 2][:, :, b % 2 * P : (b % 2 + 1) * P]
+            raw = qm_raw[b][:] if b < 2 else qm_rest[:, :, (b - 2) * P : (b - 1) * P]
             interleave(copy, grouped[:], raw)
+            qm_grouped[b] = grouped
+
+        def quantize_qm(b, codes_tag):
             qm_mx[b] = mx_pair("qm%d" % b, P, codes_tag)
-            quantize(qm_mx[b], slice(0, P), grouped[:].rearrange("p d j -> p (d j)"), E4)
+            quantize(qm_mx[b], slice(0, P), qm_grouped[b][:].rearrange("p d j -> p (d j)"), E4)
 
         def scatter(b, dk, lo, hi, tag):
             staged = keep.tile([P, hi - lo], F32, name="staged", tag=tag, align_bytes=64)
             nc.scalar.copy(staged[:], dk)
-            nc.vector.tensor_copy(windows[b][:].indirect(slots(lo, hi)), staged[:])
+            if hi - lo >= HALF:
+                nc.vector.tensor_copy(windows[b][:].indirect(slots(lo, hi)), staged[:])
+            else:
+                nc.vector.tensor_tensor(windows[b][:].indirect(slots(lo, hi)), staged[:], zeros[:], ADD)
 
         def dk_pass(b, first):
             dk = psum.tile([P, N], F32, name="dk", tag="wide", bufs=4)
@@ -185,8 +197,9 @@ def tile_attend_gat_exp_k_kernel(tc, qT, kT, vT, doT, rw, qm, offs, out):
             weights = keep.tile([P, width, PACK], F32, name="weights", tag="weights%d" % c, align_bytes=64)
             nc.scalar.activation(weights[:], scores[:].rearrange("p t i -> p i t"), ACT.Exp)
             if c == 0:
-                quantize_qm(0, "qm0", nc.scalar.copy)
-                quantize_qm(1, "q_grouped", nc.vector.tensor_copy)
+                group_qm(0, "qm0", nc.scalar.copy)
+                quantize_qm(0, None)
+                group_qm(1, "q_grouped", nc.vector.tensor_copy)
             nc.vector.tensor_tensor(ds_grouped[:, cols, :], weights[:], gated_grouped[:, cols, :], MULT)
             quantize(
                 ds_mx,
@@ -196,10 +209,12 @@ def tile_attend_gat_exp_k_kernel(tc, qT, kT, vT, doT, rw, qm, offs, out):
             )
 
         scatter(0, dk_pass(0, 0)[:, HALF:], 0, HALF, "early")
-        scatter(0, dk_pass(0, HALF)[:, HALF:], HALF, N, "late")
+        scatter(0, dk_pass(0, P)[:, N - P :], HALF, HALF + P, "middle")
+        scatter(0, dk_pass(0, HALF)[:, N - P :], HALF + P, N, "late")
         nc.sync.dma_start(out[:P, :], windows[0][:])
-        for b, tag, codes_tag in ((1, None, None), (2, "weights0", "ds_grouped"), (3, "late", None)):
+        for b, tag, codes_tag in ((1, None, "ds_grouped"), (2, "weights0", "ds_grouped"), (3, "late", None)):
             if tag:
-                quantize_qm(b, tag, nc.scalar.copy, codes_tag)
+                group_qm(b, tag, nc.scalar.copy)
+            quantize_qm(b, codes_tag)
             scatter(b, dk_pass(b, HALF)[:], 0, N, "staged%d" % b)
             nc.sync.dma_start(out[b * P : (b + 1) * P, :], windows[b][:])

@@ -14,7 +14,6 @@ E4 = mybir.dt.float8_e4m3fn_x4
 E5 = mybir.dt.float8_e5m2_x4
 ACT = mybir.ActivationFunctionType
 MULT = mybir.AluOpType.mult
-ADD = mybir.AluOpType.add
 
 P = 128
 PACK = 4
@@ -87,8 +86,6 @@ def tile_attend_gat_exp_k_kernel(tc, qT, kT, vT, doT, rw, qm, offs, out):
         ds_mx = mx_pair("ds", HALF + N)
         nc.vector.memset(ds_mx[0][:, :HALF], 0)
         nc.vector.memset(ds_mx[1][:, :HALF], 0)
-        zeros = keep.tile([P, P], F32, name="zeros")
-        nc.vector.memset(zeros[:], 0.0)
         windows = [keep.tile([P, T], F32, name="window%d" % b) for b in range(D // P)]
         for b, window in enumerate(windows):
             (nc.vector, nc.gpsimd)[b % 2].memset(window[:], 0.0)
@@ -176,10 +173,7 @@ def tile_attend_gat_exp_k_kernel(tc, qT, kT, vT, doT, rw, qm, offs, out):
         def scatter(b, dk, lo, hi, tag):
             staged = keep.tile([P, hi - lo], F32, name="staged", tag=tag, align_bytes=64)
             nc.scalar.copy(staged[:], dk)
-            if hi - lo >= HALF:
-                nc.vector.tensor_copy(windows[b][:].indirect(slots(lo, hi)), staged[:])
-            else:
-                nc.vector.tensor_tensor(windows[b][:].indirect(slots(lo, hi)), staged[:], zeros[:], ADD)
+            nc.vector.tensor_copy(windows[b][:].indirect(slots(lo, hi)), staged[:])
 
         def dk_pass(b, first):
             dk = psum.tile([P, N], F32, name="dk", tag="wide", bufs=4)
@@ -209,8 +203,7 @@ def tile_attend_gat_exp_k_kernel(tc, qT, kT, vT, doT, rw, qm, offs, out):
             )
 
         scatter(0, dk_pass(0, 0)[:, HALF:], 0, HALF, "early")
-        scatter(0, dk_pass(0, P)[:, N - P :], HALF, HALF + P, "middle")
-        scatter(0, dk_pass(0, HALF)[:, N - P :], HALF + P, N, "late")
+        scatter(0, dk_pass(0, HALF)[:, HALF:], HALF, N, "late")
         nc.sync.dma_start(out[:P, :], windows[0][:])
         for b, tag, codes_tag in ((1, None, "ds_grouped"), (2, "weights0", "ds_grouped"), (3, "late", None)):
             if tag:

@@ -166,9 +166,9 @@ def tile_attend_gat_exp_k_kernel(tc, qT, kT, vT, doT, rw, qm, offs, out):
             interleave(copy, grouped[:], raw)
             qm_grouped[b] = grouped
 
-        def quantize_qm(b, codes_tag):
-            qm_mx[b] = mx_pair("qm%d" % b, P, codes_tag)
-            quantize(qm_mx[b], slice(0, P), qm_grouped[b][:].rearrange("p d j -> p (d j)"), E4)
+        def quantize_qm(b, pair, first):
+            qm_mx[b] = (pair, slice(first, first + P))
+            quantize(*qm_mx[b], qm_grouped[b][:].rearrange("p d j -> p (d j)"), E4)
 
         def scatter(b, dk, lo, hi, tag):
             staged = keep.tile([P, hi - lo], F32, name="staged", tag=tag, align_bytes=64)
@@ -177,7 +177,7 @@ def tile_attend_gat_exp_k_kernel(tc, qT, kT, vT, doT, rw, qm, offs, out):
 
         def dk_pass(b, first):
             dk = psum.tile([P, N], F32, name="dk", tag="wide", bufs=4)
-            multiply(dk[:], qm_mx[b], slice(0, P), E4, ds_mx, slice(first, first + N), E5)
+            multiply(dk[:], *qm_mx[b], E4, ds_mx, slice(first, first + N), E5)
             return dk
 
         ds_grouped = keep.tile([P, N, PACK], BF16, name="ds_grouped", tag="ds_grouped", align_bytes=64)
@@ -192,7 +192,7 @@ def tile_attend_gat_exp_k_kernel(tc, qT, kT, vT, doT, rw, qm, offs, out):
             nc.scalar.activation(weights[:], scores[:].rearrange("p t i -> p i t"), ACT.Exp)
             if c == 0:
                 group_qm(0, "qm0", nc.scalar.copy)
-                quantize_qm(0, None)
+                quantize_qm(0, mx_pair("qm0", P), 0)
                 group_qm(1, "q_grouped", nc.vector.tensor_copy)
             nc.vector.tensor_tensor(ds_grouped[:, cols, :], weights[:], gated_grouped[:, cols, :], MULT)
             quantize(
@@ -205,9 +205,12 @@ def tile_attend_gat_exp_k_kernel(tc, qT, kT, vT, doT, rw, qm, offs, out):
         scatter(0, dk_pass(0, 0)[:, HALF:], 0, HALF, "early")
         scatter(0, dk_pass(0, HALF)[:, HALF:], HALF, N, "late")
         nc.sync.dma_start(out[:P, :], windows[0][:])
-        for b, tag, codes_tag in ((1, None, "ds_grouped"), (2, "weights0", "ds_grouped"), (3, "late", None)):
-            if tag:
-                group_qm(b, tag, nc.scalar.copy)
-            quantize_qm(b, codes_tag)
+        quantize_qm(1, mx_pair("qm1", P, "ds_grouped"), 0)
+        group_qm(2, "weights0", nc.scalar.copy)
+        group_qm(3, "weights3", nc.scalar.copy)
+        qm_late = mx_pair("qm_late", 2 * P, "late")
+        for b in (2, 3):
+            quantize_qm(b, qm_late, (b - 2) * P)
+        for b in (1, 2, 3):
             scatter(b, dk_pass(b, HALF)[:], 0, N, "staged%d" % b)
             nc.sync.dma_start(out[b * P : (b + 1) * P, :], windows[b][:])

@@ -180,7 +180,12 @@ def tile_attend_gat_exp_k_kernel(tc, qT, kT, vT, doT, rw, qm, offs, out):
             multiply(dk[:], *qm_mx[b], E4, ds_mx, slice(first, first + N), E5)
             return dk
 
-        ds_grouped = keep.tile([P, N, PACK], BF16, name="ds_grouped", tag="ds_grouped", align_bytes=64)
+        ds_grouped = {}
+
+        def quantize_ds(c):
+            lo = HALF + sum(CHUNKS[:c])
+            quantize(ds_mx, slice(lo, lo + CHUNKS[c]), ds_grouped[c][:].rearrange("p i t -> p (i t)"), E5)
+
         for c, width in enumerate(CHUNKS):
             lo = sum(CHUNKS[:c])
             cols = slice(lo, lo + width)
@@ -194,18 +199,16 @@ def tile_attend_gat_exp_k_kernel(tc, qT, kT, vT, doT, rw, qm, offs, out):
                 group_qm(0, "qm0", nc.scalar.copy)
                 quantize_qm(0, mx_pair("qm0", P), 0)
                 group_qm(1, "q_grouped", nc.vector.tensor_copy)
-            nc.vector.tensor_tensor(ds_grouped[:, cols, :], weights[:], gated_grouped[:, cols, :], MULT)
-            quantize(
-                ds_mx,
-                slice(HALF + lo, HALF + lo + width),
-                ds_grouped[:, cols, :].rearrange("p i t -> p (i t)"),
-                E5,
-            )
+            ds_grouped[c] = keep.tile([P, width, PACK], BF16, name="ds", tag="ds_grouped%d" % c, align_bytes=64)
+            nc.vector.tensor_tensor(ds_grouped[c][:], weights[:], gated_grouped[:, cols, :], MULT)
+            if c:
+                quantize_ds(c - 1)
+        quantize_ds(len(CHUNKS) - 1)
 
         scatter(0, dk_pass(0, 0)[:, HALF:], 0, HALF, "early")
         scatter(0, dk_pass(0, HALF)[:, HALF:], HALF, N, "late")
         nc.sync.dma_start(out[:P, :], windows[0][:])
-        quantize_qm(1, mx_pair("qm1", P, "ds_grouped"), 0)
+        quantize_qm(1, mx_pair("qm1", P, "ds_grouped3"), 0)
         group_qm(2, "weights0", nc.scalar.copy)
         group_qm(3, "weights3", nc.scalar.copy)
         qm_late = mx_pair("qm_late", 2 * P, "late")

@@ -57,21 +57,27 @@ def tile_attend_gat_exp_k_kernel(tc, qT, kT, vT, doT, rw, qm, offs, out):
         do_raw = keep.tile([P, PACK, R], F32, name="do_raw")
         q_early = keep.tile([P, PACK, Q_SPLIT * PACK], F32, name="q_early")
         q_late = keep.tile([P, PACK, R - Q_SPLIT * PACK], F32, name="q_late", tag="q_raw", align_bytes=64)
-        v_pool = [keep.tile([P, T], F32, name="v_pool%d" % j) for j in range(PACK)]
-        k_pool = [keep.tile([P, T], F32, name="k_pool%d" % j) for j in range(PACK)]
+        v_first = keep.tile([P, 2, T], F32, name="v_first")
+        v_last = [keep.tile([P, T], F32, name="v_pool%d" % j) for j in range(2, PACK)]
+        v_pool = [v_first[:, j, :] for j in range(2)] + [plane[:] for plane in v_last]
+        k_first = keep.tile([P, 2, T], F32, name="k_first")
+        k_last = [keep.tile([P, T], F32, name="k_pool%d" % j) for j in range(2, PACK)]
+        k_pool = [k_first[:, j, :] for j in range(2)] + [plane[:] for plane in k_last]
         qm_raw = [keep.tile([P, PACK, P], F32, name="qm_raw%d" % b) for b in range(2)]
         qm_rest = keep.tile([P, PACK, 2 * P], F32, name="qm_rest")
         v_rows = vT.rearrange("(p j) n -> p j n", j=PACK)
         k_rows = kT.rearrange("(p j) n -> p j n", j=PACK)
         qm_rows = qm[0].rearrange("(p j) d -> p j d", j=PACK)
 
-        nc.sync.dma_start(do_raw[:], doT[0].rearrange("(p j) r -> p j r", j=PACK))
         nc.sync.dma_start(offsets[:], offs)
+        nc.sync.dma_start(v_first[:], v_rows[:, :2, :])
+        nc.sync.dma_start(do_raw[:], doT[0].rearrange("(p j) r -> p j r", j=PACK))
         nc.sync.dma_start(gate[:], rw[0].rearrange("(p t) o -> p (t o)", t=PACK))
-        for j in range(PACK):
-            nc.sync.dma_start(v_pool[j][:], v_rows[:, j, :])
-        for j in range(PACK):
-            nc.sync.dma_start(k_pool[j][:], k_rows[:, j, :])
+        for j in range(2, PACK):
+            nc.sync.dma_start(v_pool[j], v_rows[:, j, :])
+        nc.sync.dma_start(k_first[:], k_rows[:, :2, :])
+        for j in range(2, PACK):
+            nc.sync.dma_start(k_pool[j], k_rows[:, j, :])
         q_rows = qT[0].rearrange("(p j) r -> p j r", j=PACK)
         nc.sync.dma_start(q_early[:], q_rows[:, :, : Q_SPLIT * PACK])
         nc.sync.dma_start(q_late[:], q_rows[:, :, Q_SPLIT * PACK :])
@@ -113,7 +119,7 @@ def tile_attend_gat_exp_k_kernel(tc, qT, kT, vT, doT, rw, qm, offs, out):
         v_grouped = keep.tile([P, N, PACK], BF16, name="v_grouped", tag="pools", align_bytes=64)
         v_listed = keep.tile([P, PACK, N], F32, name="v_listed")
         for j in range(PACK):
-            nc.vector.tensor_copy(v_listed[:, j, :], v_pool[j][:].indirect(offsets[:]))
+            nc.vector.tensor_copy(v_listed[:, j, :], v_pool[j].indirect(offsets[:]))
             if j % 2 == 1:
                 nc.vector.tensor_copy(
                     v_grouped[:, :, j - 1 : j + 1], v_listed[:, j - 1 : j + 1, :].rearrange("p j i -> p i j")
@@ -128,15 +134,15 @@ def tile_attend_gat_exp_k_kernel(tc, qT, kT, vT, doT, rw, qm, offs, out):
         gated_grouped = keep.tile([P, N, PACK], F32, name="gated_grouped")
         interleave(nc.scalar.copy, gated_grouped[:], gated[:])
 
-        k_grouped = keep.tile([P, N, PACK], BF16, name="k_grouped", align_bytes=64)
+        k_grouped = keep.tile([P, N, PACK], BF16, name="k_grouped", tag="k_grouped", align_bytes=64)
         k_listed = keep.tile([P, PACK, N], F32, name="k_listed", tag="pools", align_bytes=64)
         for j in range(PACK - 1):
-            nc.vector.tensor_copy(k_listed[:, j, :], k_pool[j][:].indirect(offsets[:]))
+            nc.vector.tensor_copy(k_listed[:, j, :], k_pool[j].indirect(offsets[:]))
             if j == 1:
                 nc.vector.tensor_copy(k_grouped[:, :, 0:2], k_listed[:, 0:2, :].rearrange("p j i -> p i j"))
         for lo in range(0, N, HALF):
             nc.vector.tensor_copy(
-                k_listed[:, PACK - 1, lo : lo + HALF], k_pool[PACK - 1][:].indirect(slots(lo, lo + HALF))
+                k_listed[:, PACK - 1, lo : lo + HALF], k_pool[PACK - 1].indirect(slots(lo, lo + HALF))
             )
         for lo, copy in ((0, nc.scalar.copy), (HALF, nc.vector.tensor_copy)):
             copy(k_grouped[:, lo : lo + HALF, 2:4], k_listed[:, 2:4, lo : lo + HALF].rearrange("p j i -> p i j"))
@@ -149,12 +155,28 @@ def tile_attend_gat_exp_k_kernel(tc, qT, kT, vT, doT, rw, qm, offs, out):
         k_mx = [quantize_keys(0, None)]
 
         q_mx = mx_pair("q", R)
-        q_grouped = group_queries(
-            [(nc.scalar.copy, q_early, 0, Q_SPLIT), (nc.vector.tensor_copy, q_late, Q_SPLIT, P)], "q_grouped"
-        )
-        for t in range(PACK):
-            quantize(q_mx, slice(t * P, (t + 1) * P), q_grouped[:, t].rearrange("p m j -> p (m j)"), E4)
-        k_mx.append(quantize_keys(HALF, "q_raw"))
+        q_grouped = [
+            keep.tile([P, 2, P, PACK], BF16, name="q_grouped%d" % u, tag="q_grouped%d" % u, align_bytes=64)
+            for u in range(2)
+        ]
+
+        def group_q(copy, raw, first, u, lo, hi):
+            copy(
+                q_grouped[u][:, :, first + lo : first + hi, :].rearrange("p t m j -> p m j t"),
+                raw[:].rearrange("p j (m t) -> p m j t", t=PACK)[:, lo:hi, :, 2 * u : 2 * u + 2],
+            )
+
+        for raw, first, most, rest in (
+            (q_early, 0, nc.scalar.copy, nc.vector.tensor_copy),
+            (q_late, Q_SPLIT, nc.vector.tensor_copy, nc.scalar.copy),
+        ):
+            group_q(most, raw, first, 0, 0, Q_SPLIT)
+            group_q(most, raw, first, 1, 0, Q_SPLIT // 2)
+            group_q(rest, raw, first, 1, Q_SPLIT // 2, Q_SPLIT)
+        quantize(q_mx, slice(0, 2 * P), q_grouped[0][:].rearrange("p t m j -> p (t m j)"), E4)
+        for t in (2, 3):
+            quantize(q_mx, slice(t * P, (t + 1) * P), q_grouped[1][:, t - 2].rearrange("p m j -> p (m j)"), E4)
+        k_mx.append(quantize_keys(HALF, "q_grouped1"))
 
         qm_mx = {}
 
@@ -162,8 +184,7 @@ def tile_attend_gat_exp_k_kernel(tc, qT, kT, vT, doT, rw, qm, offs, out):
 
         def group_qm(b, tag, copy):
             grouped = keep.tile([P, P, PACK], BF16, name="qm_grouped", tag=tag, align_bytes=64)
-            raw = qm_raw[b][:] if b < 2 else qm_rest[:, :, (b - 2) * P : (b - 1) * P]
-            interleave(copy, grouped[:], raw)
+            interleave(copy, grouped[:], qm_rest[:, :, (b - 2) * P : (b - 1) * P])
             qm_grouped[b] = grouped
 
         def quantize_qm(b, pair, first):
@@ -188,19 +209,27 @@ def tile_attend_gat_exp_k_kernel(tc, qT, kT, vT, doT, rw, qm, offs, out):
 
         for c, width in enumerate(CHUNKS):
             lo = sum(CHUNKS[:c])
-            cols = slice(lo, lo + width)
             key_cols = slice(lo % HALF, lo % HALF + width)
             scores = psum.tile([P, PACK, width], F32, name="scores", bufs=len(CHUNKS))
             for t in range(PACK):
                 multiply(scores[:, t, :], q_mx, slice(t * P, (t + 1) * P), E4, k_mx[lo // HALF], key_cols, E4)
-            weights = keep.tile([P, width, PACK], F32, name="weights", tag="weights%d" % c, align_bytes=64)
-            nc.scalar.activation(weights[:], scores[:].rearrange("p t i -> p i t"), ACT.Exp)
             if c == 0:
-                group_qm(0, "qm0", nc.scalar.copy)
-                quantize_qm(0, mx_pair("qm0", P), 0)
-                group_qm(1, "q_grouped", nc.vector.tensor_copy)
+                qm_first = keep.tile([P, 2, P, PACK], BF16, name="qm_first", align_bytes=64)
+                for b in range(2):
+                    interleave(nc.scalar.copy, qm_first[:, b], qm_raw[b][:])
+                pair = mx_pair("qm01", 2 * P, "k_grouped")
+                quantize(pair, slice(0, 2 * P), qm_first[:].rearrange("p b d j -> p (b d j)"), E4)
+                for b in range(2):
+                    qm_mx[b] = (pair, slice(b * P, (b + 1) * P))
             ds_grouped[c] = keep.tile([P, width, PACK], BF16, name="ds", tag="ds_grouped%d" % c, align_bytes=64)
-            nc.vector.tensor_tensor(ds_grouped[c][:], weights[:], gated_grouped[:, cols, :], MULT)
+            step = width // 2 if c == 0 else width
+            for at in range(0, width, step):
+                tag = "weights%d" % c if at + step == width else "weights_first"
+                weights = keep.tile([P, step, PACK], F32, name="weights", tag=tag, align_bytes=64)
+                nc.scalar.activation(weights[:], scores[:, :, at : at + step].rearrange("p t i -> p i t"), ACT.Exp)
+                nc.vector.tensor_tensor(
+                    ds_grouped[c][:, at : at + step, :], weights[:], gated_grouped[:, lo + at : lo + at + step, :], MULT
+                )
             if c:
                 quantize_ds(c - 1)
         quantize_ds(len(CHUNKS) - 1)
@@ -208,7 +237,6 @@ def tile_attend_gat_exp_k_kernel(tc, qT, kT, vT, doT, rw, qm, offs, out):
         scatter(0, dk_pass(0, 0)[:, HALF:], 0, HALF, "early")
         scatter(0, dk_pass(0, HALF)[:, HALF:], HALF, N, "late")
         nc.sync.dma_start(out[:P, :], windows[0][:])
-        quantize_qm(1, mx_pair("qm1", P, "ds_grouped3"), 0)
         group_qm(2, "weights0", nc.scalar.copy)
         group_qm(3, "weights3", nc.scalar.copy)
         qm_late = mx_pair("qm_late", 2 * P, "late")

@@ -139,13 +139,13 @@ def tile_attend_gat_exp_k_kernel(tc, qT, kT, vT, doT, rw, qm, offs, out):
         for j in range(PACK - 1):
             nc.vector.tensor_copy(k_listed[:, j, :], k_pool[j].indirect(offsets[:]))
             if j == 1:
-                nc.vector.tensor_copy(k_grouped[:, :, 0:2], k_listed[:, 0:2, :].rearrange("p j i -> p i j"))
+                nc.vector.tensor_copy(k_grouped[:, :HALF, 0:2], k_listed[:, 0:2, :HALF].rearrange("p j i -> p i j"))
         for lo in range(0, N, HALF):
             nc.vector.tensor_copy(
                 k_listed[:, PACK - 1, lo : lo + HALF], k_pool[PACK - 1].indirect(slots(lo, lo + HALF))
             )
-        for lo, copy in ((0, nc.scalar.copy), (HALF, nc.vector.tensor_copy)):
-            copy(k_grouped[:, lo : lo + HALF, 2:4], k_listed[:, 2:4, lo : lo + HALF].rearrange("p j i -> p i j"))
+        nc.scalar.copy(k_grouped[:, :HALF, 2:4], k_listed[:, 2:4, :HALF].rearrange("p j i -> p i j"))
+        interleave(nc.vector.tensor_copy, k_grouped[:, HALF:, :], k_listed[:, :, HALF:])
 
         def quantize_keys(lo, codes_tag):
             pair = mx_pair("k%d" % lo, HALF, codes_tag)
@@ -167,7 +167,7 @@ def tile_attend_gat_exp_k_kernel(tc, qT, kT, vT, doT, rw, qm, offs, out):
             )
 
         for raw, first, most, rest in (
-            (q_early, 0, nc.scalar.copy, nc.vector.tensor_copy),
+            (q_early, 0, nc.scalar.copy, nc.scalar.copy),
             (q_late, Q_SPLIT, nc.vector.tensor_copy, nc.scalar.copy),
         ):
             group_q(most, raw, first, 0, 0, Q_SPLIT)
@@ -237,7 +237,7 @@ def tile_attend_gat_exp_k_kernel(tc, qT, kT, vT, doT, rw, qm, offs, out):
         scatter(0, dk_pass(0, 0)[:, HALF:], 0, HALF, "early")
         scatter(0, dk_pass(0, HALF)[:, HALF:], HALF, N, "late")
         nc.sync.dma_start(out[:P, :], windows[0][:])
-        group_qm(2, "weights0", nc.scalar.copy)
+        group_qm(2, "weights2", nc.scalar.copy)
         group_qm(3, "weights3", nc.scalar.copy)
         qm_late = mx_pair("qm_late", 2 * P, "late")
         for b in (2, 3):

@@ -21,6 +21,7 @@ CHUNKS = (128, 128, 128, 128)
 RUN = 4
 HALF = N // 2
 STRIPE = 16
+PAD = N - CHUNKS[0]
 Q_SPLIT = 64
 
 
@@ -89,9 +90,9 @@ def tile_attend_gat_exp_k_kernel(tc, qT, kT, vT, doT, rw, qm, offs, out):
         warm_out = keep.tile([P, 8], F32, name="warm_out")
         nc.vector.memset(warm[:], 0.0)
         nc.scalar.activation(warm_out[:], warm[:], ACT.Exp)
-        ds_mx = mx_pair("ds", HALF + N)
-        nc.vector.memset(ds_mx[0][:, :HALF], 0)
-        nc.vector.memset(ds_mx[1][:, :HALF], 0)
+        ds_mx = mx_pair("ds", PAD + N)
+        nc.vector.memset(ds_mx[0][:, :PAD], 0)
+        nc.vector.memset(ds_mx[1][:, :PAD], 0)
         windows = [keep.tile([P, T], F32, name="window%d" % b) for b in range(D // P)]
         for b, window in enumerate(windows):
             (nc.vector, nc.gpsimd)[b % 2].memset(window[:], 0.0)
@@ -204,7 +205,7 @@ def tile_attend_gat_exp_k_kernel(tc, qT, kT, vT, doT, rw, qm, offs, out):
         ds_grouped = {}
 
         def quantize_ds(c):
-            lo = HALF + sum(CHUNKS[:c])
+            lo = PAD + sum(CHUNKS[:c])
             quantize(ds_mx, slice(lo, lo + CHUNKS[c]), ds_grouped[c][:].rearrange("p i t -> p (i t)"), E5)
 
         for c, width in enumerate(CHUNKS):
@@ -234,8 +235,11 @@ def tile_attend_gat_exp_k_kernel(tc, qT, kT, vT, doT, rw, qm, offs, out):
                 quantize_ds(c - 1)
         quantize_ds(len(CHUNKS) - 1)
 
-        scatter(0, dk_pass(0, 0)[:, HALF:], 0, HALF, "early")
-        scatter(0, dk_pass(0, HALF)[:, HALF:], HALF, N, "late")
+        early = keep.tile([P, HALF], F32, name="early", tag="early", align_bytes=64)
+        for c in range(2):
+            nc.scalar.copy(early[:, c * CHUNKS[0] : (c + 1) * CHUNKS[0]], dk_pass(0, c * CHUNKS[0])[:, PAD:])
+        nc.vector.tensor_copy(windows[0][:].indirect(slots(0, HALF)), early[:])
+        scatter(0, dk_pass(0, PAD)[:, HALF:], HALF, N, "late")
         nc.sync.dma_start(out[:P, :], windows[0][:])
         group_qm(2, "weights2", nc.scalar.copy)
         group_qm(3, "weights3", nc.scalar.copy)
@@ -243,5 +247,5 @@ def tile_attend_gat_exp_k_kernel(tc, qT, kT, vT, doT, rw, qm, offs, out):
         for b in (2, 3):
             quantize_qm(b, qm_late, (b - 2) * P)
         for b in (1, 2, 3):
-            scatter(b, dk_pass(b, HALF)[:], 0, N, "staged%d" % b)
+            scatter(b, dk_pass(b, PAD)[:], 0, N, "staged%d" % b)
             nc.sync.dma_start(out[b * P : (b + 1) * P, :], windows[b][:])

@@ -55,12 +55,11 @@ def tile_attend_gat_exp_k_kernel(tc, qT, kT, vT, doT, rw, qm, offs, out):
 
         offsets = keep.tile([P, N // STRIPE], U16, name="offsets")
         gate = keep.tile([P, PACK], F32, name="gate")
-        do_raw = keep.tile([P, PACK, R], F32, name="do_raw")
+        do_raw = keep.tile([P, PACK, R], F32, name="do_raw", tag="pools", align_bytes=64)
         q_early = keep.tile([P, PACK, Q_SPLIT * PACK], F32, name="q_early")
         q_late = keep.tile([P, PACK, R - Q_SPLIT * PACK], F32, name="q_late", tag="q_raw", align_bytes=64)
-        v_first = keep.tile([P, 2, T], F32, name="v_first")
-        v_last = [keep.tile([P, T], F32, name="v_pool%d" % j) for j in range(2, PACK)]
-        v_pool = [v_first[:, j, :] for j in range(2)] + [plane[:] for plane in v_last]
+        v_all = keep.tile([P, PACK, T], F32, name="v_all")
+        v_pool = [v_all[:, j, :] for j in range(PACK)]
         k_first = keep.tile([P, 2, T], F32, name="k_first")
         k_last = [keep.tile([P, T], F32, name="k_pool%d" % j) for j in range(2, PACK)]
         k_pool = [k_first[:, j, :] for j in range(2)] + [plane[:] for plane in k_last]
@@ -70,12 +69,10 @@ def tile_attend_gat_exp_k_kernel(tc, qT, kT, vT, doT, rw, qm, offs, out):
         k_rows = kT.rearrange("(p j) n -> p j n", j=PACK)
         qm_rows = qm[0].rearrange("(p j) d -> p j d", j=PACK)
 
+        nc.sync.dma_start(v_all[:], v_rows)
+        nc.scalar.dma_start(gate[:], rw[0].rearrange("(p t) o -> p (t o)", t=PACK))
         nc.sync.dma_start(offsets[:], offs)
-        nc.sync.dma_start(v_first[:], v_rows[:, :2, :])
         nc.sync.dma_start(do_raw[:], doT[0].rearrange("(p j) r -> p j r", j=PACK))
-        nc.sync.dma_start(gate[:], rw[0].rearrange("(p t) o -> p (t o)", t=PACK))
-        for j in range(2, PACK):
-            nc.sync.dma_start(v_pool[j], v_rows[:, j, :])
         nc.sync.dma_start(k_first[:], k_rows[:, :2, :])
         for j in range(2, PACK):
             nc.sync.dma_start(k_pool[j], k_rows[:, j, :])
@@ -117,30 +114,29 @@ def tile_attend_gat_exp_k_kernel(tc, qT, kT, vT, doT, rw, qm, offs, out):
         do_mx = mx_pair("do", R)
         do_grouped = group_queries([(nc.scalar.copy, do_raw, 0, P)], "do_grouped")
         quantize(do_mx, everything, do_grouped[:].rearrange("p t m j -> p (t m j)"), E5)
-        v_grouped = keep.tile([P, N, PACK], BF16, name="v_grouped", tag="pools", align_bytes=64)
+        v_grouped = [
+            keep.tile([P, HALF, PACK], BF16, name="v_grouped", tag=tag, align_bytes=64) for tag in ("v_front", "pools")
+        ]
         v_listed = keep.tile([P, PACK, N], F32, name="v_listed")
         for j in range(PACK):
             nc.vector.tensor_copy(v_listed[:, j, :], v_pool[j].indirect(offsets[:]))
-            if j % 2 == 1:
-                nc.vector.tensor_copy(
-                    v_grouped[:, :, j - 1 : j + 1], v_listed[:, j - 1 : j + 1, :].rearrange("p j i -> p i j")
-                )
         v_mx = mx_pair("v", N)
-        quantize(v_mx, everything, v_grouped[:].rearrange("p i j -> p (i j)"), E4)
+        for u, copy in enumerate((nc.vector.tensor_copy, nc.scalar.copy)):
+            half = slice(u * HALF, (u + 1) * HALF)
+            interleave(copy, v_grouped[u][:], v_listed[:, :, half])
+            quantize(v_mx, half, v_grouped[u][:].rearrange("p i j -> p (i j)"), E4)
         gated = keep.tile([P, PACK, N], F32, name="gated")
         for t in range(PACK):
             dp = psum.tile([P, N], F32, name="dp", tag="wide", bufs=4)
             multiply(dp[:], do_mx, slice(t * P, (t + 1) * P), E5, v_mx, everything, E4)
             nc.scalar.activation(gated[:, t, :], dp[:], ACT.Copy, scale=gate[:, t : t + 1])
-        gated_grouped = keep.tile([P, N, PACK], F32, name="gated_grouped")
-        interleave(nc.scalar.copy, gated_grouped[:], gated[:])
 
         k_grouped = keep.tile([P, N, PACK], BF16, name="k_grouped", tag="k_grouped", align_bytes=64)
         k_listed = keep.tile([P, PACK, N], F32, name="k_listed", tag="pools", align_bytes=64)
         for j in range(PACK - 1):
             nc.vector.tensor_copy(k_listed[:, j, :], k_pool[j].indirect(offsets[:]))
             if j == 1:
-                nc.vector.tensor_copy(k_grouped[:, :HALF, 0:2], k_listed[:, 0:2, :HALF].rearrange("p j i -> p i j"))
+                nc.scalar.copy(k_grouped[:, :HALF, 0:2], k_listed[:, 0:2, :HALF].rearrange("p j i -> p i j"))
         for lo in range(0, N, HALF):
             nc.vector.tensor_copy(
                 k_listed[:, PACK - 1, lo : lo + HALF], k_pool[PACK - 1].indirect(slots(lo, lo + HALF))
@@ -226,10 +222,13 @@ def tile_attend_gat_exp_k_kernel(tc, qT, kT, vT, doT, rw, qm, offs, out):
             step = width // 2 if c == 0 else width
             for at in range(0, width, step):
                 tag = "weights%d" % c if at + step == width else "weights_first"
-                weights = keep.tile([P, step, PACK], F32, name="weights", tag=tag, align_bytes=64)
-                nc.scalar.activation(weights[:], scores[:, :, at : at + step].rearrange("p t i -> p i t"), ACT.Exp)
+                weights = keep.tile([P, PACK, step], F32, name="weights", tag=tag, align_bytes=64)
+                nc.scalar.activation(weights[:], scores[:, :, at : at + step], ACT.Exp)
                 nc.vector.tensor_tensor(
-                    ds_grouped[c][:, at : at + step, :], weights[:], gated_grouped[:, lo + at : lo + at + step, :], MULT
+                    ds_grouped[c][:, at : at + step, :].rearrange("p (c i) t -> p c t i", i=2),
+                    weights[:].rearrange("p t (c i) -> p c t i", i=2),
+                    gated[:, :, lo + at : lo + at + step].rearrange("p t (c i) -> p c t i", i=2),
+                    MULT,
                 )
             if c:
                 quantize_ds(c - 1)

@@ -219,9 +219,9 @@ def tile_attend_gat_exp_k_kernel(tc, qT, kT, vT, doT, rw, qm, offs, out):
                 for b in range(2):
                     qm_mx[b] = (pair, slice(b * P, (b + 1) * P))
             ds_grouped[c] = keep.tile([P, width, PACK], BF16, name="ds", tag="ds_grouped%d" % c, align_bytes=64)
-            step = width // 2 if c == 0 else width
+            step = width // 2 if c < 2 else width
             for at in range(0, width, step):
-                tag = "weights%d" % c if at + step == width else "weights_first"
+                tag = "weights%d" % c if at + step == width else "weights_first%d" % c
                 weights = keep.tile([P, PACK, step], F32, name="weights", tag=tag, align_bytes=64)
                 nc.scalar.activation(weights[:], scores[:, :, at : at + step], ACT.Exp)
                 nc.vector.tensor_tensor(
@@ -230,8 +230,8 @@ def tile_attend_gat_exp_k_kernel(tc, qT, kT, vT, doT, rw, qm, offs, out):
                     gated[:, :, lo + at : lo + at + step].rearrange("p t (c i) -> p c t i", i=2),
                     MULT,
                 )
-            if c:
-                quantize_ds(c - 1)
+                if c and at == 0:
+                    quantize_ds(c - 1)
         quantize_ds(len(CHUNKS) - 1)
 
         early = keep.tile([P, HALF], F32, name="early", tag="early", align_bytes=64)

@@ -17,12 +17,12 @@ MULT = mybir.AluOpType.mult
 
 P = 128
 PACK = 4
-CHUNKS = (128, 128, 128, 128)
+CHUNK = 128
 RUN = 4
 HALF = N // 2
 STRIPE = 16
-PAD = N - CHUNKS[0]
-Q_SPLIT = 64
+SPLIT = 64
+Q_SHARE = 96
 
 
 def tile_attend_gat_exp_k_kernel(tc, qT, kT, vT, doT, rw, qm, offs, out):
@@ -55,30 +55,30 @@ def tile_attend_gat_exp_k_kernel(tc, qT, kT, vT, doT, rw, qm, offs, out):
 
         offsets = keep.tile([P, N // STRIPE], U16, name="offsets")
         gate = keep.tile([P, PACK], F32, name="gate")
-        do_raw = keep.tile([P, PACK, R], F32, name="do_raw", tag="pools", align_bytes=64)
-        q_early = keep.tile([P, PACK, Q_SPLIT * PACK], F32, name="q_early")
-        q_late = keep.tile([P, PACK, R - Q_SPLIT * PACK], F32, name="q_late", tag="q_raw", align_bytes=64)
-        v_all = keep.tile([P, PACK, T], F32, name="v_all")
-        v_pool = [v_all[:, j, :] for j in range(PACK)]
-        k_first = keep.tile([P, 2, T], F32, name="k_first")
-        k_last = [keep.tile([P, T], F32, name="k_pool%d" % j) for j in range(2, PACK)]
-        k_pool = [k_first[:, j, :] for j in range(2)] + [plane[:] for plane in k_last]
+        q_raw = keep.tile([P, PACK, R], F32, name="q_raw", tag="pools", align_bytes=64)
+        do_early = keep.tile([P, PACK, SPLIT * PACK], F32, name="do_early")
+        do_late = keep.tile([P, PACK, R - SPLIT * PACK], F32, name="do_late", tag="do_raw", align_bytes=64)
+        k_all = keep.tile([P, PACK, T], F32, name="k_all")
+        k_pool = [k_all[:, j, :] for j in range(PACK)]
+        v_first = keep.tile([P, 2, T], F32, name="v_first")
+        v_last = [keep.tile([P, T], F32, name="v_pool%d" % j) for j in range(2, PACK)]
+        v_pool = [v_first[:, j, :] for j in range(2)] + [plane[:] for plane in v_last]
         qm_raw = [keep.tile([P, PACK, P], F32, name="qm_raw%d" % b) for b in range(2)]
         qm_rest = keep.tile([P, PACK, 2 * P], F32, name="qm_rest")
         v_rows = vT.rearrange("(p j) n -> p j n", j=PACK)
         k_rows = kT.rearrange("(p j) n -> p j n", j=PACK)
         qm_rows = qm[0].rearrange("(p j) d -> p j d", j=PACK)
 
-        nc.sync.dma_start(v_all[:], v_rows)
+        nc.sync.dma_start(k_all[:], k_rows)
         nc.scalar.dma_start(gate[:], rw[0].rearrange("(p t) o -> p (t o)", t=PACK))
         nc.sync.dma_start(offsets[:], offs)
-        nc.sync.dma_start(do_raw[:], doT[0].rearrange("(p j) r -> p j r", j=PACK))
-        nc.sync.dma_start(k_first[:], k_rows[:, :2, :])
+        nc.sync.dma_start(q_raw[:], qT[0].rearrange("(p j) r -> p j r", j=PACK))
+        nc.sync.dma_start(v_first[:], v_rows[:, :2, :])
         for j in range(2, PACK):
-            nc.sync.dma_start(k_pool[j], k_rows[:, j, :])
-        q_rows = qT[0].rearrange("(p j) r -> p j r", j=PACK)
-        nc.sync.dma_start(q_early[:], q_rows[:, :, : Q_SPLIT * PACK])
-        nc.sync.dma_start(q_late[:], q_rows[:, :, Q_SPLIT * PACK :])
+            nc.sync.dma_start(v_pool[j], v_rows[:, j, :])
+        do_rows = doT[0].rearrange("(p j) r -> p j r", j=PACK)
+        nc.sync.dma_start(do_early[:], do_rows[:, :, : SPLIT * PACK])
+        nc.sync.dma_start(do_late[:], do_rows[:, :, SPLIT * PACK :])
         for b in range(2):
             nc.sync.dma_start(qm_raw[b][:], qm_rows[:, :, b * P : (b + 1) * P])
         nc.sync.dma_start(qm_rest[:], qm_rows[:, :, 2 * P :])
@@ -87,9 +87,6 @@ def tile_attend_gat_exp_k_kernel(tc, qT, kT, vT, doT, rw, qm, offs, out):
         warm_out = keep.tile([P, 8], F32, name="warm_out")
         nc.vector.memset(warm[:], 0.0)
         nc.scalar.activation(warm_out[:], warm[:], ACT.Exp)
-        ds_mx = mx_pair("ds", PAD + N)
-        nc.vector.memset(ds_mx[0][:, :PAD], 0)
-        nc.vector.memset(ds_mx[1][:, :PAD], 0)
         windows = [keep.tile([P, T], F32, name="window%d" % b) for b in range(D // P)]
         for b, window in enumerate(windows):
             (nc.vector, nc.gpsimd)[b % 2].memset(window[:], 0.0)
@@ -100,151 +97,135 @@ def tile_attend_gat_exp_k_kernel(tc, qT, kT, vT, doT, rw, qm, offs, out):
                 planes.rearrange("p j (c i) -> p c j i", i=RUN),
             )
 
-        def group_queries(shares, name):
-            grouped = keep.tile([P, PACK, P, PACK], BF16, name=name, tag=name, align_bytes=64)
-            for copy, raw, lo, hi in shares:
-                copy(
-                    grouped[:, :, lo:hi, :].rearrange("p t m j -> p m j t"),
-                    raw[:].rearrange("p j (m t) -> p m j t", t=PACK),
-                )
-            return grouped
-
         everything = slice(0, N)
 
-        do_mx = mx_pair("do", R)
-        do_grouped = group_queries([(nc.scalar.copy, do_raw, 0, P)], "do_grouped")
-        quantize(do_mx, everything, do_grouped[:].rearrange("p t m j -> p (t m j)"), E5)
-        v_grouped = [
-            keep.tile([P, HALF, PACK], BF16, name="v_grouped", tag=tag, align_bytes=64) for tag in ("v_front", "pools")
-        ]
-        v_listed = keep.tile([P, PACK, N], F32, name="v_listed")
-        for j in range(PACK):
-            nc.vector.tensor_copy(v_listed[:, j, :], v_pool[j].indirect(offsets[:]))
-        v_mx = mx_pair("v", N)
-        for u, copy in enumerate((nc.vector.tensor_copy, nc.scalar.copy)):
-            half = slice(u * HALF, (u + 1) * HALF)
-            interleave(copy, v_grouped[u][:], v_listed[:, :, half])
-            quantize(v_mx, half, v_grouped[u][:].rearrange("p i j -> p (i j)"), E4)
+        q_mx = mx_pair("q", R)
+        q_grouped = keep.tile([P, PACK, P, PACK], BF16, name="q_grouped", align_bytes=64)
+        k_grouped = keep.tile([P, N, PACK], BF16, name="k_grouped", align_bytes=64)
+        k_listed = keep.tile([P, PACK, N], F32, name="k_listed")
+        for j in range(2):
+            nc.vector.tensor_copy(k_listed[:, j, :], k_pool[j].indirect(offsets[:]))
+        nc.vector.tensor_copy(k_listed[:, 2, :HALF], k_pool[2].indirect(slots(0, HALF)))
+        nc.scalar.activation(k_listed[:, 3, :], k_pool[3].indirect(offsets[:]), ACT.Copy)
+        nc.scalar.activation(k_listed[:, 2, HALF:], k_pool[2].indirect(slots(HALF, N)), ACT.Copy)
+        k_mx = mx_pair("k", N)
+        interleave(nc.vector.tensor_copy, k_grouped[:], k_listed[:])
+        quantize(k_mx, everything, k_grouped[:].rearrange("p i j -> p (i j)"), E4)
+        for copy, lo, hi in ((nc.scalar.copy, 0, Q_SHARE), (nc.vector.tensor_copy, Q_SHARE, P)):
+            copy(
+                q_grouped[:, :, lo:hi, :].rearrange("p t m j -> p m j t"),
+                q_raw[:].rearrange("p j (m t) -> p m j t", t=PACK)[:, lo:hi],
+            )
+        quantize(q_mx, everything, q_grouped[:].rearrange("p t m j -> p (t m j)"), E4)
+        weights = keep.tile([P, PACK, N], F32, name="weights")
         gated = keep.tile([P, PACK, N], F32, name="gated")
         for t in range(PACK):
-            dp = psum.tile([P, N], F32, name="dp", tag="wide", bufs=4)
-            multiply(dp[:], do_mx, slice(t * P, (t + 1) * P), E5, v_mx, everything, E4)
-            nc.scalar.activation(gated[:, t, :], dp[:], ACT.Copy, scale=gate[:, t : t + 1])
+            scores = psum.tile([P, N], F32, name="scores", tag="wide", bufs=4)
+            multiply(scores[:], q_mx, slice(t * P, (t + 1) * P), E4, k_mx, everything, E4)
+            nc.scalar.activation(weights[:, t, :], scores[:], ACT.Exp)
+        for t in range(PACK):
+            nc.scalar.activation(gated[:, t, :], weights[:, t, :], ACT.Copy, scale=gate[:, t : t + 1])
 
-        k_grouped = keep.tile([P, N, PACK], BF16, name="k_grouped", tag="k_grouped", align_bytes=64)
-        k_listed = keep.tile([P, PACK, N], F32, name="k_listed", tag="pools", align_bytes=64)
+        v_grouped = keep.tile([P, N, PACK], BF16, name="v_grouped", tag="v_grouped", align_bytes=64)
+        v_listed = keep.tile([P, PACK, N], F32, name="v_listed", tag="pools", align_bytes=64)
         for j in range(PACK - 1):
-            nc.vector.tensor_copy(k_listed[:, j, :], k_pool[j].indirect(offsets[:]))
+            nc.vector.tensor_copy(v_listed[:, j, :], v_pool[j].indirect(offsets[:]))
             if j == 1:
-                nc.scalar.copy(k_grouped[:, :HALF, 0:2], k_listed[:, 0:2, :HALF].rearrange("p j i -> p i j"))
+                nc.scalar.copy(v_grouped[:, :HALF, 0:2], v_listed[:, 0:2, :HALF].rearrange("p j i -> p i j"))
         for lo in range(0, N, HALF):
             nc.vector.tensor_copy(
-                k_listed[:, PACK - 1, lo : lo + HALF], k_pool[PACK - 1].indirect(slots(lo, lo + HALF))
+                v_listed[:, PACK - 1, lo : lo + HALF], v_pool[PACK - 1].indirect(slots(lo, lo + HALF))
             )
-        nc.scalar.copy(k_grouped[:, :HALF, 2:4], k_listed[:, 2:4, :HALF].rearrange("p j i -> p i j"))
-        interleave(nc.vector.tensor_copy, k_grouped[:, HALF:, :], k_listed[:, :, HALF:])
+        nc.scalar.copy(v_grouped[:, :HALF, 2:4], v_listed[:, 2:4, :HALF].rearrange("p j i -> p i j"))
+        interleave(nc.vector.tensor_copy, v_grouped[:, HALF:, :], v_listed[:, :, HALF:])
 
-        def quantize_keys(lo, codes_tag):
-            pair = mx_pair("k%d" % lo, HALF, codes_tag)
-            quantize(pair, slice(0, HALF), k_grouped[:, lo : lo + HALF, :].rearrange("p i j -> p (i j)"), E4)
+        def quantize_values(lo, codes_tag):
+            pair = mx_pair("v%d" % lo, HALF, codes_tag)
+            quantize(pair, slice(0, HALF), v_grouped[:, lo : lo + HALF, :].rearrange("p i j -> p (i j)"), E4)
             return pair
 
-        k_mx = [quantize_keys(0, None)]
+        v_mx = [quantize_values(0, None)]
 
-        q_mx = mx_pair("q", R)
-        q_grouped = [
-            keep.tile([P, 2, P, PACK], BF16, name="q_grouped%d" % u, tag="q_grouped%d" % u, align_bytes=64)
+        do_mx = mx_pair("do", R)
+        do_grouped = [
+            keep.tile([P, 2, P, PACK], BF16, name="do_grouped%d" % u, tag="do_grouped%d" % u, align_bytes=64)
             for u in range(2)
         ]
 
-        def group_q(copy, raw, first, u, lo, hi):
+        def group_do(copy, raw, first, u, lo, hi):
             copy(
-                q_grouped[u][:, :, first + lo : first + hi, :].rearrange("p t m j -> p m j t"),
+                do_grouped[u][:, :, first + lo : first + hi, :].rearrange("p t m j -> p m j t"),
                 raw[:].rearrange("p j (m t) -> p m j t", t=PACK)[:, lo:hi, :, 2 * u : 2 * u + 2],
             )
 
         for raw, first, most, rest in (
-            (q_early, 0, nc.scalar.copy, nc.scalar.copy),
-            (q_late, Q_SPLIT, nc.vector.tensor_copy, nc.scalar.copy),
+            (do_early, 0, nc.scalar.copy, nc.scalar.copy),
+            (do_late, SPLIT, nc.vector.tensor_copy, nc.scalar.copy),
         ):
-            group_q(most, raw, first, 0, 0, Q_SPLIT)
-            group_q(most, raw, first, 1, 0, Q_SPLIT // 2)
-            group_q(rest, raw, first, 1, Q_SPLIT // 2, Q_SPLIT)
-        quantize(q_mx, slice(0, 2 * P), q_grouped[0][:].rearrange("p t m j -> p (t m j)"), E4)
+            group_do(most, raw, first, 0, 0, SPLIT)
+            group_do(most, raw, first, 1, 0, SPLIT // 2)
+            group_do(rest, raw, first, 1, SPLIT // 2, SPLIT)
+        quantize(do_mx, slice(0, 2 * P), do_grouped[0][:].rearrange("p t m j -> p (t m j)"), E5)
         for t in (2, 3):
-            quantize(q_mx, slice(t * P, (t + 1) * P), q_grouped[1][:, t - 2].rearrange("p m j -> p (m j)"), E4)
-        k_mx.append(quantize_keys(HALF, "q_grouped1"))
+            quantize(do_mx, slice(t * P, (t + 1) * P), do_grouped[1][:, t - 2].rearrange("p m j -> p (m j)"), E5)
+        v_mx.append(quantize_values(HALF, "do_grouped1"))
 
         qm_mx = {}
+        qm_first = keep.tile([P, 2, P, PACK], BF16, name="qm_first", align_bytes=64)
+        qm_second = keep.tile([P, 2, P, PACK], BF16, name="qm_second", align_bytes=64)
 
-        qm_grouped = {}
+        ds_mx = mx_pair("ds", N)
+        ds_grouped = {}
+        late = keep.tile([P, HALF], F32, name="late", align_bytes=64)
 
-        def group_qm(b, tag, copy):
-            grouped = keep.tile([P, P, PACK], BF16, name="qm_grouped", tag=tag, align_bytes=64)
-            interleave(copy, grouped[:], qm_rest[:, :, (b - 2) * P : (b - 1) * P])
-            qm_grouped[b] = grouped
-
-        def quantize_qm(b, pair, first):
-            qm_mx[b] = (pair, slice(first, first + P))
-            quantize(*qm_mx[b], qm_grouped[b][:].rearrange("p d j -> p (d j)"), E4)
-
-        def scatter(b, dk, lo, hi, tag):
-            staged = keep.tile([P, hi - lo], F32, name="staged", tag=tag, align_bytes=64)
-            nc.scalar.copy(staged[:], dk)
-            nc.vector.tensor_copy(windows[b][:].indirect(slots(lo, hi)), staged[:])
-
-        def dk_pass(b, first):
-            dk = psum.tile([P, N], F32, name="dk", tag="wide", bufs=4)
-            multiply(dk[:], *qm_mx[b], E4, ds_mx, slice(first, first + N), E5)
+        def dk_pass(b, lo, hi):
+            dk = psum.tile([P, hi - lo], F32, name="dk", tag="wide", bufs=4)
+            multiply(dk[:], *qm_mx[b], E4, ds_mx, slice(lo, hi), E5)
             return dk
 
-        ds_grouped = {}
+        def finish_chunk(c):
+            lo = c * CHUNK
+            quantize(ds_mx, slice(lo, lo + CHUNK), ds_grouped[c][:].rearrange("p i t -> p (i t)"), E5)
 
-        def quantize_ds(c):
-            lo = PAD + sum(CHUNKS[:c])
-            quantize(ds_mx, slice(lo, lo + CHUNKS[c]), ds_grouped[c][:].rearrange("p i t -> p (i t)"), E5)
-
-        for c, width in enumerate(CHUNKS):
-            lo = sum(CHUNKS[:c])
-            key_cols = slice(lo % HALF, lo % HALF + width)
-            scores = psum.tile([P, PACK, width], F32, name="scores", bufs=len(CHUNKS))
+        for c in range(N // CHUNK):
+            lo = c * CHUNK
+            value_cols = slice(lo % HALF, lo % HALF + CHUNK)
+            dp = psum.tile([P, PACK, CHUNK], F32, name="dp", bufs=N // CHUNK)
             for t in range(PACK):
-                multiply(scores[:, t, :], q_mx, slice(t * P, (t + 1) * P), E4, k_mx[lo // HALF], key_cols, E4)
+                multiply(dp[:, t, :], do_mx, slice(t * P, (t + 1) * P), E5, v_mx[lo // HALF], value_cols, E4)
             if c == 0:
-                qm_first = keep.tile([P, 2, P, PACK], BF16, name="qm_first", align_bytes=64)
                 for b in range(2):
                     interleave(nc.scalar.copy, qm_first[:, b], qm_raw[b][:])
-                pair = mx_pair("qm01", 2 * P, "k_grouped")
+                pair = mx_pair("qm01", 2 * P, "v_grouped")
                 quantize(pair, slice(0, 2 * P), qm_first[:].rearrange("p b d j -> p (b d j)"), E4)
                 for b in range(2):
                     qm_mx[b] = (pair, slice(b * P, (b + 1) * P))
-            ds_grouped[c] = keep.tile([P, width, PACK], BF16, name="ds", tag="ds_grouped%d" % c, align_bytes=64)
-            step = width // 2 if c < 2 else width
-            for at in range(0, width, step):
-                tag = "weights%d" % c if at + step == width else "weights_first%d" % c
-                weights = keep.tile([P, PACK, step], F32, name="weights", tag=tag, align_bytes=64)
-                nc.scalar.activation(weights[:], scores[:, :, at : at + step], ACT.Exp)
-                nc.vector.tensor_tensor(
-                    ds_grouped[c][:, at : at + step, :].rearrange("p (c i) t -> p c t i", i=2),
-                    weights[:].rearrange("p t (c i) -> p c t i", i=2),
-                    gated[:, :, lo + at : lo + at + step].rearrange("p t (c i) -> p c t i", i=2),
-                    MULT,
-                )
-                if c and at == 0:
-                    quantize_ds(c - 1)
-        quantize_ds(len(CHUNKS) - 1)
+            ds_grouped[c] = keep.tile([P, CHUNK, PACK], BF16, name="ds", tag="ds_grouped%d" % c, align_bytes=64)
+            nc.vector.tensor_tensor(
+                ds_grouped[c][:].rearrange("p (c i) t -> p c t i", i=2),
+                dp[:].rearrange("p t (c i) -> p c t i", i=2),
+                gated[:, :, lo : lo + CHUNK].rearrange("p t (c i) -> p c t i", i=2),
+                MULT,
+            )
+            if c:
+                finish_chunk(c - 1)
+        finish_chunk(N // CHUNK - 1)
 
-        early = keep.tile([P, HALF], F32, name="early", tag="early", align_bytes=64)
-        for c in range(2):
-            nc.scalar.copy(early[:, c * CHUNKS[0] : (c + 1) * CHUNKS[0]], dk_pass(0, c * CHUNKS[0])[:, PAD:])
-        nc.vector.tensor_copy(windows[0][:].indirect(slots(0, HALF)), early[:])
-        scatter(0, dk_pass(0, PAD)[:, HALF:], HALF, N, "late")
+        early = keep.tile([P, HALF], F32, name="early", tag="ds_grouped2", align_bytes=64)
+        nc.scalar.copy(early[:], dk_pass(0, 0, HALF)[:])
+        for lo in range(HALF, N, CHUNK):
+            nc.scalar.copy(late[:, lo - HALF : lo - HALF + CHUNK], dk_pass(0, lo, lo + CHUNK)[:])
+        for u, piece in enumerate((early, late)):
+            nc.vector.tensor_copy(windows[0][:].indirect(slots(u * HALF, (u + 1) * HALF)), piece[:])
         nc.sync.dma_start(out[:P, :], windows[0][:])
-        group_qm(2, "weights2", nc.scalar.copy)
-        group_qm(3, "weights3", nc.scalar.copy)
+        for b in range(2):
+            interleave(nc.scalar.copy, qm_second[:, b], qm_rest[:, :, b * P : (b + 1) * P])
         qm_late = mx_pair("qm_late", 2 * P, "late")
+        quantize(qm_late, slice(0, 2 * P), qm_second[:].rearrange("p b d j -> p (b d j)"), E4)
         for b in (2, 3):
-            quantize_qm(b, qm_late, (b - 2) * P)
+            qm_mx[b] = (qm_late, slice((b - 2) * P, (b - 1) * P))
         for b in (1, 2, 3):
-            scatter(b, dk_pass(b, PAD)[:], 0, N, "staged%d" % b)
+            whole = keep.tile([P, N], F32, name="staged%d" % b, align_bytes=64)
+            nc.scalar.copy(whole[:], dk_pass(b, 0, N)[:])
+            nc.vector.tensor_copy(windows[b][:].indirect(offsets[:]), whole[:])
             nc.sync.dma_start(out[b * P : (b + 1) * P, :], windows[b][:])

@@ -22,7 +22,7 @@ RUN = 4
 HALF = N // 2
 STRIPE = 16
 SPLIT = 64
-Q_SHARE = 96
+V_SHARE = 448
 
 
 def tile_attend_gat_exp_k_kernel(tc, qT, kT, vT, doT, rw, qm, offs, out):
@@ -61,7 +61,7 @@ def tile_attend_gat_exp_k_kernel(tc, qT, kT, vT, doT, rw, qm, offs, out):
         k_all = keep.tile([P, PACK, T], F32, name="k_all")
         k_pool = [k_all[:, j, :] for j in range(PACK)]
         v_first = keep.tile([P, 2, T], F32, name="v_first")
-        v_last = [keep.tile([P, T], F32, name="v_pool%d" % j) for j in range(2, PACK)]
+        v_last = [keep.tile([P, T], F32, name="v_pool", tag="v_pool%d" % j) for j in range(2, PACK)]
         v_pool = [v_first[:, j, :] for j in range(2)] + [plane[:] for plane in v_last]
         qm_raw = [keep.tile([P, PACK, P], F32, name="qm_raw%d" % b) for b in range(2)]
         qm_rest = keep.tile([P, PACK, 2 * P], F32, name="qm_rest")
@@ -100,7 +100,6 @@ def tile_attend_gat_exp_k_kernel(tc, qT, kT, vT, doT, rw, qm, offs, out):
         everything = slice(0, N)
 
         q_mx = mx_pair("q", R)
-        q_grouped = keep.tile([P, PACK, P, PACK], BF16, name="q_grouped", align_bytes=64)
         k_grouped = keep.tile([P, N, PACK], BF16, name="k_grouped", align_bytes=64)
         k_listed = keep.tile([P, PACK, N], F32, name="k_listed")
         for j in range(2):
@@ -111,33 +110,34 @@ def tile_attend_gat_exp_k_kernel(tc, qT, kT, vT, doT, rw, qm, offs, out):
         k_mx = mx_pair("k", N)
         interleave(nc.vector.tensor_copy, k_grouped[:], k_listed[:])
         quantize(k_mx, everything, k_grouped[:].rearrange("p i j -> p (i j)"), E4)
-        for copy, lo, hi in ((nc.scalar.copy, 0, Q_SHARE), (nc.vector.tensor_copy, Q_SHARE, P)):
-            copy(
-                q_grouped[:, :, lo:hi, :].rearrange("p t m j -> p m j t"),
-                q_raw[:].rearrange("p j (m t) -> p m j t", t=PACK)[:, lo:hi],
+        for u in range(2):
+            q_grouped = keep.tile([P, 2, P, PACK], BF16, name="q_grouped%d" % u, align_bytes=64)
+            nc.scalar.copy(
+                q_grouped[:].rearrange("p t m j -> p m j t"),
+                q_raw[:].rearrange("p j (m t) -> p m j t", t=PACK)[:, :, :, 2 * u : 2 * u + 2],
             )
-        quantize(q_mx, everything, q_grouped[:].rearrange("p t m j -> p (t m j)"), E4)
+            quantize(q_mx, slice(2 * u * P, 2 * (u + 1) * P), q_grouped[:].rearrange("p t m j -> p (t m j)"), E4)
         weights = keep.tile([P, PACK, N], F32, name="weights")
-        gated = keep.tile([P, PACK, N], F32, name="gated")
         for t in range(PACK):
             scores = psum.tile([P, N], F32, name="scores", tag="wide", bufs=4)
             multiply(scores[:], q_mx, slice(t * P, (t + 1) * P), E4, k_mx, everything, E4)
             nc.scalar.activation(weights[:, t, :], scores[:], ACT.Exp)
-        for t in range(PACK):
-            nc.scalar.activation(gated[:, t, :], weights[:, t, :], ACT.Copy, scale=gate[:, t : t + 1])
 
         v_grouped = keep.tile([P, N, PACK], BF16, name="v_grouped", tag="v_grouped", align_bytes=64)
         v_listed = keep.tile([P, PACK, N], F32, name="v_listed", tag="pools", align_bytes=64)
         for j in range(PACK - 1):
             nc.vector.tensor_copy(v_listed[:, j, :], v_pool[j].indirect(offsets[:]))
-            if j == 1:
-                nc.scalar.copy(v_grouped[:, :HALF, 0:2], v_listed[:, 0:2, :HALF].rearrange("p j i -> p i j"))
-        for lo in range(0, N, HALF):
-            nc.vector.tensor_copy(
-                v_listed[:, PACK - 1, lo : lo + HALF], v_pool[PACK - 1].indirect(slots(lo, lo + HALF))
-            )
-        nc.scalar.copy(v_grouped[:, :HALF, 2:4], v_listed[:, 2:4, :HALF].rearrange("p j i -> p i j"))
-        interleave(nc.vector.tensor_copy, v_grouped[:, HALF:, :], v_listed[:, :, HALF:])
+        gated = keep.tile([P, PACK, N], F32, name="gated", tag="v_pool2")
+        for t in range(PACK):
+            nc.vector.tensor_scalar_mul(gated[:, t, :], weights[:, t, :], gate[:, t : t + 1])
+        nc.vector.tensor_copy(v_listed[:, PACK - 1, :HALF], v_pool[PACK - 1].indirect(slots(0, HALF)))
+        nc.scalar.activation(v_listed[:, PACK - 1, HALF:], v_pool[PACK - 1].indirect(slots(HALF, N)), ACT.Copy)
+        for copy, lo, hi in (
+            (nc.vector.tensor_copy, 0, HALF),
+            (nc.vector.tensor_copy, HALF, V_SHARE),
+            (nc.scalar.copy, V_SHARE, N),
+        ):
+            interleave(copy, v_grouped[:, lo:hi, :], v_listed[:, :, lo:hi])
 
         def quantize_values(lo, codes_tag):
             pair = mx_pair("v%d" % lo, HALF, codes_tag)
@@ -168,7 +168,7 @@ def tile_attend_gat_exp_k_kernel(tc, qT, kT, vT, doT, rw, qm, offs, out):
         quantize(do_mx, slice(0, 2 * P), do_grouped[0][:].rearrange("p t m j -> p (t m j)"), E5)
         for t in (2, 3):
             quantize(do_mx, slice(t * P, (t + 1) * P), do_grouped[1][:, t - 2].rearrange("p m j -> p (m j)"), E5)
-        v_mx.append(quantize_values(HALF, "do_grouped1"))
+        v_mx.append(quantize_values(HALF, "do_grouped0"))
 
         qm_mx = {}
         qm_first = keep.tile([P, 2, P, PACK], BF16, name="qm_first", align_bytes=64)
@@ -196,10 +196,8 @@ def tile_attend_gat_exp_k_kernel(tc, qT, kT, vT, doT, rw, qm, offs, out):
             if c == 0:
                 for b in range(2):
                     interleave(nc.scalar.copy, qm_first[:, b], qm_raw[b][:])
-                pair = mx_pair("qm01", 2 * P, "v_grouped")
-                quantize(pair, slice(0, 2 * P), qm_first[:].rearrange("p b d j -> p (b d j)"), E4)
-                for b in range(2):
-                    qm_mx[b] = (pair, slice(b * P, (b + 1) * P))
+                qm_mx[0] = (mx_pair("qm0", P), slice(0, P))
+                quantize(*qm_mx[0], qm_first[:, 0].rearrange("p d j -> p (d j)"), E4)
             ds_grouped[c] = keep.tile([P, CHUNK, PACK], BF16, name="ds", tag="ds_grouped%d" % c, align_bytes=64)
             nc.vector.tensor_tensor(
                 ds_grouped[c][:].rearrange("p (c i) t -> p c t i", i=2),
@@ -210,6 +208,8 @@ def tile_attend_gat_exp_k_kernel(tc, qT, kT, vT, doT, rw, qm, offs, out):
             if c:
                 finish_chunk(c - 1)
         finish_chunk(N // CHUNK - 1)
+        qm_mx[1] = (mx_pair("qm1", P, "do_grouped0"), slice(0, P))
+        quantize(*qm_mx[1], qm_first[:, 1].rearrange("p d j -> p (d j)"), E4)
 
         early = keep.tile([P, HALF], F32, name="early", tag="ds_grouped2", align_bytes=64)
         nc.scalar.copy(early[:], dk_pass(0, 0, HALF)[:])

@@ -23,6 +23,7 @@ HALF = N // 2
 STRIPE = 16
 SPLIT = 64
 V_SHARE = 448
+LATE_SHARE = 20
 
 
 def tile_attend_gat_exp_k_kernel(tc, qT, kT, vT, doT, rw, qm, offs, out):
@@ -163,8 +164,8 @@ def tile_attend_gat_exp_k_kernel(tc, qT, kT, vT, doT, rw, qm, offs, out):
             (do_late, SPLIT, nc.vector.tensor_copy, nc.scalar.copy),
         ):
             group_do(most, raw, first, 0, 0, SPLIT)
-            group_do(most, raw, first, 1, 0, SPLIT // 2)
-            group_do(rest, raw, first, 1, SPLIT // 2, SPLIT)
+            group_do(most, raw, first, 1, 0, LATE_SHARE)
+            group_do(rest, raw, first, 1, LATE_SHARE, SPLIT)
         quantize(do_mx, slice(0, 2 * P), do_grouped[0][:].rearrange("p t m j -> p (t m j)"), E5)
         for t in (2, 3):
             quantize(do_mx, slice(t * P, (t + 1) * P), do_grouped[1][:, t - 2].rearrange("p m j -> p (m j)"), E5)
@@ -211,10 +212,10 @@ def tile_attend_gat_exp_k_kernel(tc, qT, kT, vT, doT, rw, qm, offs, out):
         qm_mx[1] = (mx_pair("qm1", P, "do_grouped0"), slice(0, P))
         quantize(*qm_mx[1], qm_first[:, 1].rearrange("p d j -> p (d j)"), E4)
 
-        early = keep.tile([P, HALF], F32, name="early", tag="ds_grouped2", align_bytes=64)
-        nc.scalar.copy(early[:], dk_pass(0, 0, HALF)[:])
-        for lo in range(HALF, N, CHUNK):
-            nc.scalar.copy(late[:, lo - HALF : lo - HALF + CHUNK], dk_pass(0, lo, lo + CHUNK)[:])
+        early = keep.tile([P, HALF], F32, name="early", align_bytes=64)
+        for lo in range(0, N, CHUNK):
+            piece = (early, late)[lo // HALF]
+            nc.scalar.copy(piece[:, lo % HALF : lo % HALF + CHUNK], dk_pass(0, lo, lo + CHUNK)[:])
         for u, piece in enumerate((early, late)):
             nc.vector.tensor_copy(windows[0][:].indirect(slots(u * HALF, (u + 1) * HALF)), piece[:])
         nc.sync.dma_start(out[:P, :], windows[0][:])

@@ -24,6 +24,7 @@ STRIPE = 16
 SPLIT = 64
 V_SHARE = 448
 LATE_SHARE = 20
+LINE = 256
 
 
 def tile_attend_gat_exp_k_kernel(tc, qT, kT, vT, doT, rw, qm, offs, out):
@@ -56,16 +57,16 @@ def tile_attend_gat_exp_k_kernel(tc, qT, kT, vT, doT, rw, qm, offs, out):
 
         offsets = keep.tile([P, N // STRIPE], U16, name="offsets")
         gate = keep.tile([P, PACK], F32, name="gate")
-        q_raw = keep.tile([P, PACK, R], F32, name="q_raw", tag="pools", align_bytes=64)
-        do_early = keep.tile([P, PACK, SPLIT * PACK], F32, name="do_early")
-        do_late = keep.tile([P, PACK, R - SPLIT * PACK], F32, name="do_late", tag="do_raw", align_bytes=64)
-        k_all = keep.tile([P, PACK, T], F32, name="k_all")
+        q_raw = keep.tile([P, PACK, R], F32, name="q_raw", tag="pools", align_bytes=LINE)
+        do_early = keep.tile([P, PACK, SPLIT * PACK], F32, name="do_early", align_bytes=LINE)
+        do_late = keep.tile([P, PACK, R - SPLIT * PACK], F32, name="do_late", tag="do_raw", align_bytes=LINE)
+        k_all = keep.tile([P, PACK, T], F32, name="k_all", align_bytes=LINE)
         k_pool = [k_all[:, j, :] for j in range(PACK)]
-        v_first = keep.tile([P, 2, T], F32, name="v_first")
-        v_last = [keep.tile([P, T], F32, name="v_pool", tag="v_pool%d" % j) for j in range(2, PACK)]
+        v_first = keep.tile([P, 2, T], F32, name="v_first", align_bytes=LINE)
+        v_last = [keep.tile([P, T], F32, name="v_pool", tag="v_pool%d" % j, align_bytes=LINE) for j in range(2, PACK)]
         v_pool = [v_first[:, j, :] for j in range(2)] + [plane[:] for plane in v_last]
-        qm_raw = [keep.tile([P, PACK, P], F32, name="qm_raw%d" % b) for b in range(2)]
-        qm_rest = keep.tile([P, PACK, 2 * P], F32, name="qm_rest")
+        qm_raw = [keep.tile([P, PACK, P], F32, name="qm_raw%d" % b, align_bytes=LINE) for b in range(2)]
+        qm_rest = keep.tile([P, PACK, 2 * P], F32, name="qm_rest", align_bytes=LINE)
         v_rows = vT.rearrange("(p j) n -> p j n", j=PACK)
         k_rows = kT.rearrange("(p j) n -> p j n", j=PACK)
         qm_rows = qm[0].rearrange("(p j) d -> p j d", j=PACK)
@@ -88,7 +89,7 @@ def tile_attend_gat_exp_k_kernel(tc, qT, kT, vT, doT, rw, qm, offs, out):
         warm_out = keep.tile([P, 8], F32, name="warm_out")
         nc.vector.memset(warm[:], 0.0)
         nc.scalar.activation(warm_out[:], warm[:], ACT.Exp)
-        windows = [keep.tile([P, T], F32, name="window%d" % b) for b in range(D // P)]
+        windows = [keep.tile([P, T], F32, name="window%d" % b, align_bytes=LINE) for b in range(D // P)]
         for b, window in enumerate(windows):
             (nc.vector, nc.gpsimd)[b % 2].memset(window[:], 0.0)
 
@@ -125,10 +126,10 @@ def tile_attend_gat_exp_k_kernel(tc, qT, kT, vT, doT, rw, qm, offs, out):
             nc.scalar.activation(weights[:, t, :], scores[:], ACT.Exp)
 
         v_grouped = keep.tile([P, N, PACK], BF16, name="v_grouped", tag="v_grouped", align_bytes=64)
-        v_listed = keep.tile([P, PACK, N], F32, name="v_listed", tag="pools", align_bytes=64)
+        v_listed = keep.tile([P, PACK, N], F32, name="v_listed", tag="pools", align_bytes=LINE)
         for j in range(PACK - 1):
             nc.vector.tensor_copy(v_listed[:, j, :], v_pool[j].indirect(offsets[:]))
-        gated = keep.tile([P, PACK, N], F32, name="gated", tag="v_pool2")
+        gated = keep.tile([P, PACK, N], F32, name="gated", tag="v_pool2", align_bytes=LINE)
         for t in range(PACK):
             nc.vector.tensor_scalar_mul(gated[:, t, :], weights[:, t, :], gate[:, t : t + 1])
         nc.vector.tensor_copy(v_listed[:, PACK - 1, :HALF], v_pool[PACK - 1].indirect(slots(0, HALF)))

@@ -23,7 +23,8 @@ HALF = N // 2
 STRIPE = 16
 SPLIT = 64
 V_SHARE = 448
-LATE_SHARE = 20
+EARLY_SHARES = (0, 32)
+LATE_SHARES = (48, 40)
 LINE = 256
 
 
@@ -129,24 +130,28 @@ def tile_attend_gat_exp_k_kernel(tc, qT, kT, vT, doT, rw, qm, offs, out):
         v_listed = keep.tile([P, PACK, N], F32, name="v_listed", tag="pools", align_bytes=LINE)
         for j in range(PACK - 1):
             nc.vector.tensor_copy(v_listed[:, j, :], v_pool[j].indirect(offsets[:]))
-        gated = keep.tile([P, PACK, N], F32, name="gated", tag="v_pool2", align_bytes=LINE)
+        gated = keep.tile([P, PACK, N], F32, name="gated")
         for t in range(PACK):
-            nc.vector.tensor_scalar_mul(gated[:, t, :], weights[:, t, :], gate[:, t : t + 1])
-        nc.vector.tensor_copy(v_listed[:, PACK - 1, :HALF], v_pool[PACK - 1].indirect(slots(0, HALF)))
+            nc.scalar.activation(gated[:, t, :], weights[:, t, :], ACT.Copy, scale=gate[:, t : t + 1])
+        for lo in (0, CHUNK):
+            nc.vector.tensor_copy(
+                v_listed[:, PACK - 1, lo : lo + CHUNK], v_pool[PACK - 1].indirect(slots(lo, lo + CHUNK))
+            )
         nc.scalar.activation(v_listed[:, PACK - 1, HALF:], v_pool[PACK - 1].indirect(slots(HALF, N)), ACT.Copy)
         for copy, lo, hi in (
-            (nc.vector.tensor_copy, 0, HALF),
+            (nc.vector.tensor_copy, 0, CHUNK),
+            (nc.vector.tensor_copy, CHUNK, HALF),
             (nc.vector.tensor_copy, HALF, V_SHARE),
             (nc.scalar.copy, V_SHARE, N),
         ):
             interleave(copy, v_grouped[:, lo:hi, :], v_listed[:, :, lo:hi])
 
-        def quantize_values(lo, codes_tag):
-            pair = mx_pair("v%d" % lo, HALF, codes_tag)
-            quantize(pair, slice(0, HALF), v_grouped[:, lo : lo + HALF, :].rearrange("p i j -> p (i j)"), E4)
-            return pair
+        def quantize_values(lo, hi, codes_tag):
+            pair = mx_pair("v%d" % lo, hi - lo, codes_tag)
+            quantize(pair, slice(0, hi - lo), v_grouped[:, lo:hi, :].rearrange("p i j -> p (i j)"), E4)
+            return [(pair, slice(c, c + CHUNK)) for c in range(0, hi - lo, CHUNK)]
 
-        v_mx = [quantize_values(0, None)]
+        v_mx = quantize_values(0, CHUNK, None)
 
         do_mx = mx_pair("do", R)
         do_grouped = [
@@ -160,17 +165,16 @@ def tile_attend_gat_exp_k_kernel(tc, qT, kT, vT, doT, rw, qm, offs, out):
                 raw[:].rearrange("p j (m t) -> p m j t", t=PACK)[:, lo:hi, :, 2 * u : 2 * u + 2],
             )
 
-        for raw, first, most, rest in (
-            (do_early, 0, nc.scalar.copy, nc.scalar.copy),
-            (do_late, SPLIT, nc.vector.tensor_copy, nc.scalar.copy),
-        ):
-            group_do(most, raw, first, 0, 0, SPLIT)
-            group_do(most, raw, first, 1, 0, LATE_SHARE)
-            group_do(rest, raw, first, 1, LATE_SHARE, SPLIT)
+        for raw, first, shares in ((do_early, 0, EARLY_SHARES), (do_late, SPLIT, LATE_SHARES)):
+            for u, share in enumerate(shares):
+                if share:
+                    group_do(nc.vector.tensor_copy, raw, first, u, 0, share)
+                group_do(nc.scalar.copy, raw, first, u, share, SPLIT)
         quantize(do_mx, slice(0, 2 * P), do_grouped[0][:].rearrange("p t m j -> p (t m j)"), E5)
         for t in (2, 3):
             quantize(do_mx, slice(t * P, (t + 1) * P), do_grouped[1][:, t - 2].rearrange("p m j -> p (m j)"), E5)
-        v_mx.append(quantize_values(HALF, "do_grouped0"))
+        v_mx.extend(quantize_values(CHUNK, HALF, "do_grouped0"))
+        v_mx.extend(quantize_values(HALF, N, "do_grouped1"))
 
         qm_mx = {}
         qm_first = keep.tile([P, 2, P, PACK], BF16, name="qm_first", align_bytes=64)
@@ -191,15 +195,16 @@ def tile_attend_gat_exp_k_kernel(tc, qT, kT, vT, doT, rw, qm, offs, out):
 
         for c in range(N // CHUNK):
             lo = c * CHUNK
-            value_cols = slice(lo % HALF, lo % HALF + CHUNK)
             dp = psum.tile([P, PACK, CHUNK], F32, name="dp", bufs=N // CHUNK)
             for t in range(PACK):
-                multiply(dp[:, t, :], do_mx, slice(t * P, (t + 1) * P), E5, v_mx[lo // HALF], value_cols, E4)
+                multiply(dp[:, t, :], do_mx, slice(t * P, (t + 1) * P), E5, *v_mx[c], E4)
             if c == 0:
-                for b in range(2):
-                    interleave(nc.scalar.copy, qm_first[:, b], qm_raw[b][:])
                 qm_mx[0] = (mx_pair("qm0", P), slice(0, P))
-                quantize(*qm_mx[0], qm_first[:, 0].rearrange("p d j -> p (d j)"), E4)
+                for d in (0, SPLIT):
+                    piece = qm_first[:, 0, d : d + SPLIT]
+                    interleave(nc.scalar.copy, piece, qm_raw[0][:, :, d : d + SPLIT])
+                    quantize(qm_mx[0][0], slice(d, d + SPLIT), piece.rearrange("p d j -> p (d j)"), E4)
+                interleave(nc.scalar.copy, qm_first[:, 1], qm_raw[1][:])
             ds_grouped[c] = keep.tile([P, CHUNK, PACK], BF16, name="ds", tag="ds_grouped%d" % c, align_bytes=64)
             nc.vector.tensor_tensor(
                 ds_grouped[c][:].rearrange("p (c i) t -> p c t i", i=2),
@@ -210,7 +215,7 @@ def tile_attend_gat_exp_k_kernel(tc, qT, kT, vT, doT, rw, qm, offs, out):
             if c:
                 finish_chunk(c - 1)
         finish_chunk(N // CHUNK - 1)
-        qm_mx[1] = (mx_pair("qm1", P, "do_grouped0"), slice(0, P))
+        qm_mx[1] = (mx_pair("qm1", P, "do_grouped1"), slice(0, P))
         quantize(*qm_mx[1], qm_first[:, 1].rearrange("p d j -> p (d j)"), E4)
 
         early = keep.tile([P, HALF], F32, name="early", align_bytes=64)

@@ -66,8 +66,11 @@ def tile_attend_gat_exp_k_kernel(tc, qT, kT, vT, doT, rw, qm, offs, out):
         v_first = keep.tile([P, 2, T], F32, name="v_first", align_bytes=LINE)
         v_last = [keep.tile([P, T], F32, name="v_pool", tag="v_pool%d" % j, align_bytes=LINE) for j in range(2, PACK)]
         v_pool = [v_first[:, j, :] for j in range(2)] + [plane[:] for plane in v_last]
-        qm_raw = [keep.tile([P, PACK, P], F32, name="qm_raw%d" % b, align_bytes=LINE) for b in range(2)]
-        qm_rest = keep.tile([P, PACK, 2 * P], F32, name="qm_rest", align_bytes=LINE)
+        qm_loads = [
+            (lo, hi, keep.tile([P, PACK, (hi - lo) * P], F32, name="qm_load%d" % lo, align_bytes=LINE))
+            for lo, hi in ((0, 1), (1, 3), (3, 4))
+        ]
+        qm_raw = [tile[:, :, (b - lo) * P : (b - lo + 1) * P] for lo, hi, tile in qm_loads for b in range(lo, hi)]
         v_rows = vT.rearrange("(p j) n -> p j n", j=PACK)
         k_rows = kT.rearrange("(p j) n -> p j n", j=PACK)
         qm_rows = qm[0].rearrange("(p j) d -> p j d", j=PACK)
@@ -82,9 +85,8 @@ def tile_attend_gat_exp_k_kernel(tc, qT, kT, vT, doT, rw, qm, offs, out):
         do_rows = doT[0].rearrange("(p j) r -> p j r", j=PACK)
         nc.sync.dma_start(do_early[:], do_rows[:, :, : SPLIT * PACK])
         nc.sync.dma_start(do_late[:], do_rows[:, :, SPLIT * PACK :])
-        for b in range(2):
-            nc.sync.dma_start(qm_raw[b][:], qm_rows[:, :, b * P : (b + 1) * P])
-        nc.sync.dma_start(qm_rest[:], qm_rows[:, :, 2 * P :])
+        for lo, hi, tile in qm_loads:
+            nc.sync.dma_start(tile[:], qm_rows[:, :, lo * P : hi * P])
 
         warm = keep.tile([P, 8], F32, name="warm")
         warm_out = keep.tile([P, 8], F32, name="warm_out")
@@ -178,7 +180,6 @@ def tile_attend_gat_exp_k_kernel(tc, qT, kT, vT, doT, rw, qm, offs, out):
 
         qm_mx = {}
         qm_first = keep.tile([P, 2, P, PACK], BF16, name="qm_first", align_bytes=64)
-        qm_second = keep.tile([P, 2, P, PACK], BF16, name="qm_second", align_bytes=64)
 
         ds_mx = mx_pair("ds", N)
         ds_grouped = {}
@@ -204,7 +205,7 @@ def tile_attend_gat_exp_k_kernel(tc, qT, kT, vT, doT, rw, qm, offs, out):
                     piece = qm_first[:, 0, d : d + SPLIT]
                     interleave(nc.scalar.copy, piece, qm_raw[0][:, :, d : d + SPLIT])
                     quantize(qm_mx[0][0], slice(d, d + SPLIT), piece.rearrange("p d j -> p (d j)"), E4)
-                interleave(nc.scalar.copy, qm_first[:, 1], qm_raw[1][:])
+                interleave(nc.scalar.copy, qm_first[:, 1], qm_raw[1])
             ds_grouped[c] = keep.tile([P, CHUNK, PACK], BF16, name="ds", tag="ds_grouped%d" % c, align_bytes=64)
             nc.vector.tensor_tensor(
                 ds_grouped[c][:].rearrange("p (c i) t -> p c t i", i=2),
@@ -225,13 +226,17 @@ def tile_attend_gat_exp_k_kernel(tc, qT, kT, vT, doT, rw, qm, offs, out):
         for u, piece in enumerate((early, late)):
             nc.vector.tensor_copy(windows[0][:].indirect(slots(u * HALF, (u + 1) * HALF)), piece[:])
         nc.sync.dma_start(out[:P, :], windows[0][:])
-        for b in range(2):
-            interleave(nc.scalar.copy, qm_second[:, b], qm_rest[:, :, b * P : (b + 1) * P])
-        qm_late = mx_pair("qm_late", 2 * P, "late")
-        quantize(qm_late, slice(0, 2 * P), qm_second[:].rearrange("p b d j -> p (b d j)"), E4)
-        for b in (2, 3):
-            qm_mx[b] = (qm_late, slice((b - 2) * P, (b - 1) * P))
+
+        def late_block(b, grouped_tag, codes_tag):
+            grouped = keep.tile([P, P, PACK], BF16, name="qm_grouped%d" % b, tag=grouped_tag, align_bytes=64)
+            interleave(nc.scalar.copy, grouped[:], qm_raw[b])
+            qm_mx[b] = (mx_pair("qm%d" % b, P, codes_tag), slice(0, P))
+            quantize(*qm_mx[b], grouped[:].rearrange("p d j -> p (d j)"), E4)
+
+        late_block(2, "qm_grouped2", "early")
         for b in (1, 2, 3):
+            if b == 2:
+                late_block(3, "late", None)
             whole = keep.tile([P, N], F32, name="staged%d" % b, align_bytes=64)
             nc.scalar.copy(whole[:], dk_pass(b, 0, N)[:])
             nc.vector.tensor_copy(windows[b][:].indirect(offsets[:]), whole[:])

from contextlib import ExitStack

import concourse.mybir as mybir

N, T, D, R = 512, 2048, 512, 512
FLOPS = 3 * 2 * N * D * R

F32 = mybir.dt.float32
BF16 = mybir.dt.bfloat16
U32 = mybir.dt.uint32
U16 = mybir.dt.uint16
U8 = mybir.dt.uint8
E4 = mybir.dt.float8_e4m3fn_x4
E5 = mybir.dt.float8_e5m2_x4
ACT = mybir.ActivationFunctionType
MULT = mybir.AluOpType.mult

P = 128
PACK = 4
CHUNK = 128
RUN = 4
HALF = N // 2
STRIPE = 16
SPLIT = 64
V_SHARE = 448
EARLY_SHARES = (0, 32)
LATE_SHARES = (48, 40)
LINE = 256


def tile_attend_gat_exp_k_kernel(tc, qT, kT, vT, doT, rw, qm, offs, out):
    nc = tc.nc
    with ExitStack() as ctx:
        keep = ctx.enter_context(tc.tile_pool(name="keep", bufs=1))
        psum = ctx.enter_context(tc.psum_pool(name="psum", bufs=1))

        def mx_pair(name, width, tag=None):
            codes = keep.tile([P, width], U32, name=name + "_codes", tag=tag or name + "_codes", align_bytes=64)
            scales = keep.tile([P, width], U8, name=name + "_scales", align_bytes=64)
            return codes, scales

        def quantize(pair, cols, grouped, fmt):
            nc.vector.quantize_mx(out=pair[0][:, cols].bitcast(fmt), scales=pair[1][:, cols], in_=grouped)

        def multiply(acc, left, left_cols, left_fmt, right, right_cols, right_fmt):
            nc.tensor.matmul_mx(
                out=acc,
                lhsT=left[0][:, left_cols].bitcast(left_fmt),
                lhsT_scale=left[1][:, left_cols],
                rhs=right[0][:, right_cols].bitcast(right_fmt),
                rhs_scale=right[1][:, right_cols],
                start=True,
                stop=True,
            )

        def slots(lo, hi):
            return offsets[:, lo // STRIPE : hi // STRIPE]

        offsets = keep.tile([P, N // STRIPE], U16, name="offsets")
        gate = keep.tile([P, PACK], F32, name="gate")
        q_raw = keep.tile([P, PACK, R], F32, name="q_raw", tag="pools", align_bytes=LINE)
        do_early = keep.tile([P, PACK, SPLIT * PACK], F32, name="do_early", align_bytes=LINE)
        do_late = keep.tile([P, PACK, R - SPLIT * PACK], F32, name="do_late", tag="do_raw", align_bytes=LINE)
        k_all = keep.tile([P, PACK, T], F32, name="k_all", align_bytes=LINE)
        k_pool = [k_all[:, j, :] for j in range(PACK)]
        v_first = keep.tile([P, 2, T], F32, name="v_first", align_bytes=LINE)
        v_last = [keep.tile([P, T], F32, name="v_pool", tag="v_pool%d" % j, align_bytes=LINE) for j in range(2, PACK)]
        v_pool = [v_first[:, j, :] for j in range(2)] + [plane[:] for plane in v_last]
        qm_loads = [
            (lo, hi, keep.tile([P, PACK, (hi - lo) * P], F32, name="qm_load%d" % lo, align_bytes=LINE))
            for lo, hi in ((0, 1), (1, 3), (3, 4))
        ]
        qm_raw = [tile[:, :, (b - lo) * P : (b - lo + 1) * P] for lo, hi, tile in qm_loads for b in range(lo, hi)]
        v_rows = vT.rearrange("(p j) n -> p j n", j=PACK)
        k_rows = kT.rearrange("(p j) n -> p j n", j=PACK)
        qm_rows = qm[0].rearrange("(p j) d -> p j d", j=PACK)

        nc.sync.dma_start(k_all[:], k_rows)
        nc.scalar.dma_start(gate[:], rw[0].rearrange("(p t) o -> p (t o)", t=PACK))
        nc.sync.dma_start(offsets[:], offs)
        nc.sync.dma_start(q_raw[:], qT[0].rearrange("(p j) r -> p j r", j=PACK))
        nc.sync.dma_start(v_first[:], v_rows[:, :2, :])
        for j in range(2, PACK):
            nc.sync.dma_start(v_pool[j], v_rows[:, j, :])
        do_rows = doT[0].rearrange("(p j) r -> p j r", j=PACK)
        nc.sync.dma_start(do_early[:], do_rows[:, :, : SPLIT * PACK])
        nc.sync.dma_start(do_late[:], do_rows[:, :, SPLIT * PACK :])
        for lo, hi, tile in qm_loads:
            nc.sync.dma_start(tile[:], qm_rows[:, :, lo * P : hi * P])

        warm = keep.tile([P, 8], F32, name="warm")
        warm_out = keep.tile([P, 8], F32, name="warm_out")
        nc.vector.memset(warm[:], 0.0)
        nc.scalar.activation(warm_out[:], warm[:], ACT.Exp)
        windows = [keep.tile([P, T], F32, name="window%d" % b, align_bytes=LINE) for b in range(D // P)]
        for b, window in enumerate(windows):
            (nc.vector, nc.gpsimd)[b % 2].memset(window[:], 0.0)

        def interleave(copy, grouped, planes):
            copy(
                grouped.rearrange("p (c i) j -> p c j i", i=RUN),
                planes.rearrange("p j (c i) -> p c j i", i=RUN),
            )

        everything = slice(0, N)

        q_mx = mx_pair("q", R)
        k_grouped = keep.tile([P, N, PACK], BF16, name="k_grouped", align_bytes=64)
        k_listed = keep.tile([P, PACK, N], F32, name="k_listed")
        for j in range(2):
            nc.vector.tensor_copy(k_listed[:, j, :], k_pool[j].indirect(offsets[:]))
        nc.vector.tensor_copy(k_listed[:, 2, :HALF], k_pool[2].indirect(slots(0, HALF)))
        nc.scalar.activation(k_listed[:, 3, :], k_pool[3].indirect(offsets[:]), ACT.Copy)
        nc.scalar.activation(k_listed[:, 2, HALF:], k_pool[2].indirect(slots(HALF, N)), ACT.Copy)
        k_mx = mx_pair("k", N)
        interleave(nc.vector.tensor_copy, k_grouped[:], k_listed[:])
        quantize(k_mx, everything, k_grouped[:].rearrange("p i j -> p (i j)"), E4)
        for u in range(2):
            q_grouped = keep.tile([P, 2, P, PACK], BF16, name="q_grouped%d" % u, align_bytes=64)
            nc.scalar.copy(
                q_grouped[:].rearrange("p t m j -> p m j t"),
                q_raw[:].rearrange("p j (m t) -> p m j t", t=PACK)[:, :, :, 2 * u : 2 * u + 2],
            )
            quantize(q_mx, slice(2 * u * P, 2 * (u + 1) * P), q_grouped[:].rearrange("p t m j -> p (t m j)"), E4)
        weights = keep.tile([P, PACK, N], F32, name="weights")
        for t in range(PACK):
            scores = psum.tile([P, N], F32, name="scores", tag="wide", bufs=4)
            multiply(scores[:], q_mx, slice(t * P, (t + 1) * P), E4, k_mx, everything, E4)
            nc.scalar.activation(weights[:, t, :], scores[:], ACT.Exp)

        v_grouped = keep.tile([P, N, PACK], BF16, name="v_grouped", tag="v_grouped", align_bytes=64)
        v_listed = keep.tile([P, PACK, N], F32, name="v_listed", tag="pools", align_bytes=LINE)
        for j in range(PACK - 1):
            nc.vector.tensor_copy(v_listed[:, j, :], v_pool[j].indirect(offsets[:]))
        gated = keep.tile([P, PACK, N], F32, name="gated")
        for t in range(PACK):
            nc.scalar.activation(gated[:, t, :], weights[:, t, :], ACT.Copy, scale=gate[:, t : t + 1])
        for lo in (0, CHUNK):
            nc.vector.tensor_copy(
                v_listed[:, PACK - 1, lo : lo + CHUNK], v_pool[PACK - 1].indirect(slots(lo, lo + CHUNK))
            )
        nc.scalar.activation(v_listed[:, PACK - 1, HALF:], v_pool[PACK - 1].indirect(slots(HALF, N)), ACT.Copy)
        for copy, lo, hi in (
            (nc.vector.tensor_copy, 0, CHUNK),
            (nc.vector.tensor_copy, CHUNK, HALF),
            (nc.vector.tensor_copy, HALF, V_SHARE),
            (nc.scalar.copy, V_SHARE, N),
        ):
            interleave(copy, v_grouped[:, lo:hi, :], v_listed[:, :, lo:hi])

        def quantize_values(lo, hi, codes_tag):
            pair = mx_pair("v%d" % lo, hi - lo, codes_tag)
            quantize(pair, slice(0, hi - lo), v_grouped[:, lo:hi, :].rearrange("p i j -> p (i j)"), E4)
            return [(pair, slice(c, c + CHUNK)) for c in range(0, hi - lo, CHUNK)]

        v_mx = quantize_values(0, CHUNK, None)

        do_mx = mx_pair("do", R)
        do_grouped = [
            keep.tile([P, 2, P, PACK], BF16, name="do_grouped%d" % u, tag="do_grouped%d" % u, align_bytes=64)
            for u in range(2)
        ]

        def group_do(copy, raw, first, u, lo, hi):
            copy(
                do_grouped[u][:, :, first + lo : first + hi, :].rearrange("p t m j -> p m j t"),
                raw[:].rearrange("p j (m t) -> p m j t", t=PACK)[:, lo:hi, :, 2 * u : 2 * u + 2],
            )

        for raw, first, shares in ((do_early, 0, EARLY_SHARES), (do_late, SPLIT, LATE_SHARES)):
            for u, share in enumerate(shares):
                if share:
                    group_do(nc.vector.tensor_copy, raw, first, u, 0, share)
                group_do(nc.scalar.copy, raw, first, u, share, SPLIT)
        quantize(do_mx, slice(0, 2 * P), do_grouped[0][:].rearrange("p t m j -> p (t m j)"), E5)
        for t in (2, 3):
            quantize(do_mx, slice(t * P, (t + 1) * P), do_grouped[1][:, t - 2].rearrange("p m j -> p (m j)"), E5)
        v_mx.extend(quantize_values(CHUNK, HALF, "do_grouped0"))
        v_mx.extend(quantize_values(HALF, N, "do_grouped1"))

        qm_mx = {}
        qm_first = keep.tile([P, 2, P, PACK], BF16, name="qm_first", align_bytes=64)

        ds_mx = mx_pair("ds", N)
        ds_grouped = {}
        late = keep.tile([P, HALF], F32, name="late", align_bytes=64)

        def dk_pass(b, lo, hi):
            dk = psum.tile([P, hi - lo], F32, name="dk", tag="wide", bufs=4)
            multiply(dk[:], *qm_mx[b], E4, ds_mx, slice(lo, hi), E5)
            return dk

        def finish_chunk(c):
            lo = c * CHUNK
            quantize(ds_mx, slice(lo, lo + CHUNK), ds_grouped[c][:].rearrange("p i t -> p (i t)"), E5)

        for c in range(N // CHUNK):
            lo = c * CHUNK
            dp = psum.tile([P, PACK, CHUNK], F32, name="dp", bufs=N // CHUNK)
            for t in range(PACK):
                multiply(dp[:, t, :], do_mx, slice(t * P, (t + 1) * P), E5, *v_mx[c], E4)
            if c == 0:
                qm_mx[0] = (mx_pair("qm0", P), slice(0, P))
                for d in (0, SPLIT):
                    piece = qm_first[:, 0, d : d + SPLIT]
                    interleave(nc.scalar.copy, piece, qm_raw[0][:, :, d : d + SPLIT])
                    quantize(qm_mx[0][0], slice(d, d + SPLIT), piece.rearrange("p d j -> p (d j)"), E4)
                interleave(nc.scalar.copy, qm_first[:, 1], qm_raw[1])
            ds_grouped[c] = keep.tile([P, CHUNK, PACK], BF16, name="ds", tag="ds_grouped%d" % c, align_bytes=64)
            nc.vector.tensor_tensor(
                ds_grouped[c][:].rearrange("p (c i) t -> p c t i", i=2),
                dp[:].rearrange("p t (c i) -> p c t i", i=2),
                gated[:, :, lo : lo + CHUNK].rearrange("p t (c i) -> p c t i", i=2),
                MULT,
            )
            if c:
                finish_chunk(c - 1)
        finish_chunk(N // CHUNK - 1)
        qm_mx[1] = (mx_pair("qm1", P, "do_grouped1"), slice(0, P))
        quantize(*qm_mx[1], qm_first[:, 1].rearrange("p d j -> p (d j)"), E4)

        early = keep.tile([P, HALF], F32, name="early", align_bytes=64)
        for lo in range(0, N, CHUNK):
            piece = (early, late)[lo // HALF]
            nc.scalar.copy(piece[:, lo % HALF : lo % HALF + CHUNK], dk_pass(0, lo, lo + CHUNK)[:])
        for u, piece in enumerate((early, late)):
            nc.vector.tensor_copy(windows[0][:].indirect(slots(u * HALF, (u + 1) * HALF)), piece[:])
        nc.sync.dma_start(out[:P, :], windows[0][:])

        def late_block(b, grouped_tag, codes_tag):
            grouped = keep.tile([P, P, PACK], BF16, name="qm_grouped%d" % b, tag=grouped_tag, align_bytes=64)
            interleave(nc.scalar.copy, grouped[:], qm_raw[b])
            qm_mx[b] = (mx_pair("qm%d" % b, P, codes_tag), slice(0, P))
            quantize(*qm_mx[b], grouped[:].rearrange("p d j -> p (d j)"), E4)

        late_block(2, "qm_grouped2", "early")
        for b in (1, 2, 3):
            if b == 2:
                late_block(3, "late", None)
            whole = keep.tile([P, N], F32, name="staged%d" % b, align_bytes=64)
            nc.scalar.copy(whole[:], dk_pass(b, 0, N)[:])
            nc.vector.tensor_copy(windows[b][:].indirect(offsets[:]), whole[:])
            nc.sync.dma_start(out[b * P : (b + 1) * P, :], windows[b][:])
